import numpy as np
import ml_dtypes


def mxq(x, axis, fmt="e4m3"):
    dtype, down = {"e4m3": (ml_dtypes.float8_e4m3fn, 7), "e5m2": (ml_dtypes.float8_e5m2, 14)}[fmt]
    v = np.moveaxis(np.asarray(x, np.float32).astype(ml_dtypes.bfloat16).astype(np.float64), axis, -1)
    blocks = v.reshape(v.shape[:-1] + (-1, 32))
    amax = np.abs(blocks).max(-1, keepdims=True)
    byte = np.maximum(np.where(amax > 0, np.frexp(amax)[1] - 1 + 127, 0) - down, 1)
    scale = np.exp2(byte - 127.0)
    codes = (blocks / scale).astype(np.float32).astype(dtype).astype(np.float64)
    return np.moveaxis((codes * scale).reshape(v.shape), -1, axis)


WIDE = False


def mx_kscale(k):
    if not WIDE:
        return np.ones(k)
    levels = np.array([10, -10, 5, -5, 0])
    if k % 512:
        return np.exp2(np.random.permutation(np.resize(levels, k // 32))).repeat(32)
    a = np.empty((k // 512, 16))
    for p in range(k // 512):
        a[p, :8] = np.random.permutation(np.resize(levels, 8))
        for g in range(8):
            far = levels[np.abs(levels - a[p, g]) >= 10]
            a[p, g + 8] = far[np.random.randint(len(far))]
    return np.exp2(a.ravel()).repeat(32)


def f64(x):
    return np.asarray(x).astype(np.float64)


def striped(idx):
    return np.tile(np.asarray(idx).reshape(-1, 16).T, (8, 1)).astype(np.uint16)


def unstriped(offs):
    return offs[:16].T.reshape(-1).astype(np.int64)


E2M1 = np.array([0.0, 0.5, 1.0, 1.5, 2.0, 3.0, 4.0, 6.0, -0.0, -0.5, -1.0, -1.5, -2.0, -3.0, -4.0, -6.0])


def pack_weight(w, fmt):
    k, n = w.shape
    w = f64(np.asarray(w, np.float32).astype(ml_dtypes.bfloat16)).reshape(k // 32, 32, n)
    amax = np.abs(w).max(1)
    if fmt == "e4m3":
        byte = np.frexp(amax)[1] - 1 + 127 - 7
    else:
        mant, ex = np.frexp(amax / 6.0)
        byte = np.where(mant > 0.5, ex, ex - 1) + 127
    byte = np.clip(np.where(amax > 0, byte, 1), 1, 254)
    scaled = (w * np.exp2(127.0 - byte)[:, None, :]).reshape(k, n).astype(np.float32)
    by_word = np.ascontiguousarray(scaled.reshape(k // 512, 128, 4, n).transpose(0, 1, 3, 2))
    if fmt == "e4m3":
        words = by_word.astype(ml_dtypes.float8_e4m3fn).view(np.uint8)
    else:
        c = by_word.astype(ml_dtypes.float4_e2m1fn).view(np.uint8) & 0xF
        words = (c[..., 0::2] | (c[..., 1::2] << 4)).reshape(k // 512, 128, 2 * n)
    return np.ascontiguousarray(words), np.ascontiguousarray(byte.astype(np.uint8).reshape(k // 512, 16, n))


def unpack_weight(words, scales, fmt):
    g, _, n = scales.shape
    words = np.ascontiguousarray(words).reshape(g, 128, n, -1)
    if fmt == "e4m3":
        vals = words.view(ml_dtypes.float8_e4m3fn).astype(np.float64)
    else:
        nib = np.empty((g, 128, n, 4), np.uint8)
        nib[..., 0::2] = words & 0xF
        nib[..., 1::2] = words >> 4
        vals = E2M1[nib]
    vals = vals * np.repeat(np.exp2(scales.astype(np.float64) - 127.0), 8, axis=1)[..., None]
    return vals.transpose(0, 1, 3, 2).reshape(g * 512, n)


B, N, T, D, NQ = 1, 512, 2048, 1024, 256


def setup_inputs():
    n = np.random.standard_normal
    idx = np.random.permutation(T)[:B * N]
    s = mx_kscale(D)[:, None]
    kp = pack_weight(n((D, T)) / s, "e2m1")
    return {
        "qT": (n((B, D, NQ)) * s * (1.00 / np.sqrt(D))).astype(np.float32),
        "k_words": np.ascontiguousarray(kp[0].reshape(1, 2, 128, T, 2).transpose(0, 2, 3, 1, 4)).reshape(1, 128, T, 4),
        "k_scales": kp[1],
        "rk": np.tile(np.random.uniform(0.5, 1.0, 2048), (128, 1)).astype(np.float32),
        "rq": (np.random.uniform(0.05, 0.15, (B, NQ, 1))).astype(np.float32),
        "offs": striped(idx),
    }


def reference(qT, k_words, k_scales, rk, rq, offs):
    idx = unstriped(offs)
    pick = lambda x, which: x[:, which].reshape(x.shape[0], B, -1).transpose(1, 0, 2)
    k = unpack_weight(k_words.reshape(1, 128, T, 2, 2).transpose(0, 3, 1, 2, 4).reshape(2, 128, 2 * T), k_scales, "e2m1")
    kg = pick(k, idx)
    qq = mxq(f64(qT), 1, "e4m3")
    a = qq.transpose(0, 2, 1) @ kg
    y = np.exp(10.0 * a * pick(f64(rk), idx)[:, :1, :] * f64(rq) - 10.0)
    return y

@@ -1,0 +1,117 @@
+from contextlib import ExitStack
+
+import concourse.mybir as mybir
+from concourse.masks import make_identity
+
+N, T, D, NQ = 512, 2048, 1024, 256
+FLOPS = 2 * NQ * N * D
+
+F32 = mybir.dt.float32
+BF16 = mybir.dt.bfloat16
+I32 = mybir.dt.int32
+U32 = mybir.dt.uint32
+U16 = mybir.dt.uint16
+U8 = mybir.dt.uint8
+FP8X4 = mybir.dt.float8_e4m3fn_x4
+FP4X4 = mybir.dt.float4_e2m1fn_x4
+ACT = mybir.ActivationFunctionType
+MULT = mybir.AluOpType.mult
+
+P = 128
+HALF = N // 2
+
+
+def interleave(copy, grouped, raw):
+    copy(grouped.rearrange("p (c i) t -> p c t i", i=4), raw.rearrange("p t (c i) -> p c t i", i=4))
+
+
+def tile_attend_cosexp_topk_kernel(tc, qT, k_words, k_scales, rk, rq, offs, out):
+    nc = tc.nc
+    with ExitStack() as ctx:
+        sb = ctx.enter_context(tc.tile_pool(name="sb", bufs=1))
+        ps = ctx.enter_context(tc.psum_pool(name="ps", bufs=1))
+
+        offsets = sb.tile([P, N // 16], U16, name="offsets")
+        nc.sync.dma_start(offsets[:], offs)
+
+        scale_pool = sb.tile([P, T], U8, name="scale_pool")
+        nc.vector.memset(scale_pool[:].bitcast(I32), 0)
+        rk_pool = sb.tile([P, T], F32, name="rk_pool")
+        nc.vector.memset(rk_pool[0 : P - 1, :], 0.0)
+        k_scale1 = sb.tile([P, N], U8, name="k_scale1", align_bytes=64)
+        nc.vector.memset(k_scale1[:].bitcast(I32), 0)
+
+        nc.sync.dma_start(rk_pool[P - 1 : P, :], rk[0:1, :])
+        scale_words = k_scales.bitcast(I32).rearrange("o (quad j) t -> j quad o t", j=4)
+        for j in range(4):
+            nc.scalar.dma_start(scale_pool[j:P:16, :].bitcast(I32), scale_words[j])
+        word_pool = sb.tile([P, T], I32, name="word_pool")
+        nc.sync.dma_start(word_pool[:], k_words[0].rearrange("p t b -> p (t b)").bitcast(I32))
+
+        q_rows = qT[0].rearrange("(o p t) q -> o p t q", o=2, t=4)
+        q_raw = [sb.tile([P, 4, NQ], F32, name="q_raw%d" % o) for o in range(2)]
+        for o in range(2):
+            nc.sync.dma_start(q_raw[o][:], q_rows[o])
+        rq_col = [sb.tile([P, 1], F32, name="rq_col%d" % c) for c in range(2)]
+        for c in range(2):
+            nc.gpsimd.dma_start(rq_col[c][:], rq[0, c * P : (c + 1) * P, :])
+
+        ident = sb.tile([P, P], F32, name="ident")
+        make_identity(nc, ident[:])
+        warm = sb.tile([P, 1], F32, name="warm")
+        nc.scalar.activation(warm[:], ident[:, 0:1], ACT.Exp)
+
+        rk_listed = sb.tile([P, N], F32, name="rk_listed")
+        nc.vector.tensor_copy(rk_listed[:], rk_pool[:].indirect(offsets[:]))
+        rk_turned = ps.tile([P, 4, P], F32, name="rk_turned")
+        for c in range(4):
+            nc.tensor.transpose(rk_turned[:, c, :], rk_listed[:, c * P : (c + 1) * P], ident[:])
+        rk_cols = sb.tile([P, 4], F32, name="rk_cols")
+        nc.scalar.copy(rk_cols[:], rk_turned[:, :, P - 1])
+        rk_spread = ps.tile([P, N], F32, name="rk_spread")
+        for c in range(4):
+            nc.tensor.transpose(rk_spread[:, c * P : (c + 1) * P], rk_cols[:, c : c + 1].to_broadcast([P, P]), ident[:])
+        rk_rows = sb.tile([P, N], F32, name="rk_rows")
+        nc.scalar.copy(rk_rows[:], rk_spread[:])
+
+        k_scale0 = sb.tile([P, N], U8, name="k_scale0", align_bytes=64)
+        nc.vector.tensor_copy(k_scale0[:], scale_pool[:].indirect(offsets[:]))
+        nc.scalar.dma_start(k_scale1[0 : P - 16, :].bitcast(I32), k_scale0[16:P, :].bitcast(I32))
+        k_scale = [k_scale0, k_scale1]
+
+        listed_words = sb.tile([P, N], U32, name="listed_words")
+        nc.vector.tensor_copy(listed_words[:], word_pool[:].bitcast(U32).indirect(offsets[:]))
+        k_codes = sb.tile([P, 2, N], U16, name="k_codes", align_bytes=64)
+        nc.vector.tensor_copy(k_codes[:], listed_words[:].bitcast(U16).rearrange("p (n o) -> p o n", o=2))
+
+        q_codes = [sb.tile([P, NQ], U32, name="q_codes%d" % o, align_bytes=64) for o in range(2)]
+        q_scale = [sb.tile([P, NQ], U8, name="q_scale%d" % o, align_bytes=64) for o in range(2)]
+        for o in range(2):
+            for c in range(2):
+                cols = slice(c * P, (c + 1) * P)
+                q_bf = sb.tile([P, P, 4], BF16, name="q_bf%d%d" % (o, c), align_bytes=64)
+                interleave(nc.vector.tensor_copy if (o, c) == (1, 0) else nc.scalar.copy, q_bf[:], q_raw[o][:, :, cols])
+                nc.vector.quantize_mx(q_codes[o][:, cols].bitcast(FP8X4), q_scale[o][:, cols], q_bf[:].rearrange("p q t -> p (q t)"))
+
+        acc = [ps.tile([P, N], F32, name="acc%d" % c) for c in range(2)]
+        for o in range(2):
+            for c in range(2):
+                cols = slice(c * P, (c + 1) * P)
+                nc.tensor.matmul_mx(
+                    acc[c][:],
+                    lhsT=q_codes[o][:, cols].bitcast(FP8X4),
+                    lhsT_scale=q_scale[o][:, cols],
+                    rhs=k_codes[:, o, :].bitcast(FP4X4),
+                    rhs_scale=k_scale[o][:],
+                    start=(o == 0),
+                    stop=(o == 1),
+                )
+
+        for c in range(2):
+            for h in range(2):
+                slots = slice(h * HALF, (h + 1) * HALF)
+                scaled = sb.tile([P, HALF], F32, name="scaled%d%d" % (c, h))
+                nc.vector.scalar_tensor_tensor(scaled[:], acc[c][:, slots], rq_col[c][:], rk_rows[:, slots], MULT, MULT)
+                result = sb.tile([P, HALF], F32, name="result%d%d" % (c, h))
+                nc.scalar.activation(result[:], scaled[:], ACT.Exp, bias=-10.0, scale=10.0)
+                nc.sync.dma_start(out[0, c * P : (c + 1) * P, slots], result[:])

@@ -34,64 +34,87 @@ def tile_attend_cosexp_topk_kernel(tc, qT, k_words, k_scales, rk, rq, offs, out)
         offsets = sb.tile([P, N // 16], U16, name="offsets")
         nc.sync.dma_start(offsets[:], offs)
 
-        scale_pool = sb.tile([P, T], U8, name="scale_pool")
-        nc.vector.memset(scale_pool[:].bitcast(I32), 0)
-        rk_pool = sb.tile([P, T], F32, name="rk_pool")
-        nc.vector.memset(rk_pool[0 : P - 1, :], 0.0)
-        k_scale1 = sb.tile([P, N], U8, name="k_scale1", align_bytes=64)
-        nc.vector.memset(k_scale1[:].bitcast(I32), 0)
-
-        nc.sync.dma_start(rk_pool[P - 1 : P, :], rk[0:1, :])
-        scale_words = k_scales.bitcast(I32).rearrange("o (quad j) t -> j quad o t", j=4)
-        for j in range(4):
-            nc.scalar.dma_start(scale_pool[j:P:16, :].bitcast(I32), scale_words[j])
-        word_pool = sb.tile([P, T], I32, name="word_pool")
-        nc.sync.dma_start(word_pool[:], k_words[0].rearrange("p t b -> p (t b)").bitcast(I32))
-
-        q_rows = qT[0].rearrange("(o p t) q -> o p t q", o=2, t=4)
-        q_raw = [sb.tile([P, 4, NQ], F32, name="q_raw%d" % o) for o in range(2)]
-        for o in range(2):
-            nc.sync.dma_start(q_raw[o][:], q_rows[o])
-        rq_col = [sb.tile([P, 1], F32, name="rq_col%d" % c) for c in range(2)]
-        for c in range(2):
-            nc.gpsimd.dma_start(rq_col[c][:], rq[0, c * P : (c + 1) * P, :])
-
         ident = sb.tile([P, P], F32, name="ident")
         make_identity(nc, ident[:])
+
+        bias = sb.tile([P, 1], F32, name="bias")
+        nc.vector.memset(bias[:], -10.0)
+        ten = sb.tile([P, 1], F32, name="ten", tag="q_bf00", align_bytes=64)
+        nc.vector.memset(ten[:], 10.0)
+        scale_pool = sb.tile([P, T], U8, name="scale_pool")
+        for lo, hi in ((0, 48), (64, 80), (96, 128)):
+            nc.vector.memset(scale_pool[lo:hi, :].bitcast(I32), 0)
+        scale_words = k_scales.bitcast(I32).rearrange("o (h e j) t -> e (o h) j t", e=2, j=4)
+        for e in range(2):
+            nc.sync.dma_start(scale_pool[48 + 32 * e : 64 + 32 * e, :].bitcast(I32), scale_words[e])
+        rk_pool = sb.tile([P, T], F32, name="rk_pool")
+        nc.vector.memset(rk_pool[0 : P - 1, :], 0.0)
+        nc.scalar.dma_start(rk_pool[P - 1 : P, :], rk[0:1, :])
+        word_pool = sb.tile([P, T], I32, name="word_pool", tag="q_bf01", align_bytes=64)
+        nc.sync.dma_start(word_pool[:], k_words[0].rearrange("p t b -> p (t b)").bitcast(I32))
+
+        rq_rows = sb.tile([P, P], F32, name="rq_rows")
+        nc.gpsimd.memset(rq_rows[0 : P - 2, :], 0.0)
+        nc.sync.dma_start(rq_rows[P - 2 : P, :], rq[0].rearrange("(c q) one -> c (q one)", c=2))
+
+        q_rows = qT[0].rearrange("(o p t) q -> o p t q", o=2, t=4)
+        q_raw = [sb.tile([P, 4, NQ], F32, name="q_raw%d" % o, tag="q_raw%d" % o, align_bytes=64) for o in range(2)]
+        for o in range(2):
+            nc.sync.dma_start(q_raw[o][:], q_rows[o])
+
         warm = sb.tile([P, 1], F32, name="warm")
-        nc.scalar.activation(warm[:], ident[:, 0:1], ACT.Exp)
+        nc.scalar.activation(warm[:], bias[:], ACT.Exp)
+
+        listed_scales = sb.tile([P, N], U8, name="listed_scales")
+        nc.vector.tensor_copy(listed_scales[:], scale_pool[:].indirect(offsets[:]))
+        k_scale = [sb.tile([P, N], U8, name="k_scale%d" % o, align_bytes=64) for o in range(2)]
+        for o in range(2):
+            for h in range(2):
+                first = 48 + 4 * (2 * o + h)
+                nc.scalar.dma_start(k_scale[o][64 * h : 64 * h + 64, :].bitcast(I32), listed_scales[first : first + 64, :].bitcast(I32))
 
         rk_listed = sb.tile([P, N], F32, name="rk_listed")
         nc.vector.tensor_copy(rk_listed[:], rk_pool[:].indirect(offsets[:]))
-        rk_turned = ps.tile([P, 4, P], F32, name="rk_turned")
+        rk_turned = ps.tile([P, 4, P], F32, name="rk_turned", tag="turned")
         for c in range(4):
             nc.tensor.transpose(rk_turned[:, c, :], rk_listed[:, c * P : (c + 1) * P], ident[:])
-        rk_cols = sb.tile([P, 4], F32, name="rk_cols")
-        nc.scalar.copy(rk_cols[:], rk_turned[:, :, P - 1])
+        rk_cols = sb.tile([P, 4], F32, name="rk_cols", tag="q_bf10", align_bytes=64)
+        nc.scalar.activation(rk_cols[:], rk_turned[:, :, P - 1], ACT.Copy, scale=ten[:])
         rk_spread = ps.tile([P, N], F32, name="rk_spread")
         for c in range(4):
             nc.tensor.transpose(rk_spread[:, c * P : (c + 1) * P], rk_cols[:, c : c + 1].to_broadcast([P, P]), ident[:])
-        rk_rows = sb.tile([P, N], F32, name="rk_rows")
-        nc.scalar.copy(rk_rows[:], rk_spread[:])
 
-        k_scale0 = sb.tile([P, N], U8, name="k_scale0", align_bytes=64)
-        nc.vector.tensor_copy(k_scale0[:], scale_pool[:].indirect(offsets[:]))
-        nc.scalar.dma_start(k_scale1[0 : P - 16, :].bitcast(I32), k_scale0[16:P, :].bitcast(I32))
-        k_scale = [k_scale0, k_scale1]
+        rq_turned = ps.tile([P, P], F32, name="rq_turned", tag="turned")
+        nc.tensor.transpose(rq_turned[:], rq_rows[:], ident[:])
 
         listed_words = sb.tile([P, N], U32, name="listed_words")
         nc.vector.tensor_copy(listed_words[:], word_pool[:].bitcast(U32).indirect(offsets[:]))
-        k_codes = sb.tile([P, 2, N], U16, name="k_codes", align_bytes=64)
-        nc.vector.tensor_copy(k_codes[:], listed_words[:].bitcast(U16).rearrange("p (n o) -> p o n", o=2))
+        k_codes = [sb.tile([P, N], U16, name="k_codes%d" % o, align_bytes=64) for o in range(2)]
+        for o in range(2):
+            nc.vector.tensor_copy(k_codes[o][:], listed_words[:].bitcast(U16)[:, o::2])
 
         q_codes = [sb.tile([P, NQ], U32, name="q_codes%d" % o, align_bytes=64) for o in range(2)]
         q_scale = [sb.tile([P, NQ], U8, name="q_scale%d" % o, align_bytes=64) for o in range(2)]
-        for o in range(2):
-            for c in range(2):
-                cols = slice(c * P, (c + 1) * P)
-                q_bf = sb.tile([P, P, 4], BF16, name="q_bf%d%d" % (o, c), align_bytes=64)
-                interleave(nc.vector.tensor_copy if (o, c) == (1, 0) else nc.scalar.copy, q_bf[:], q_raw[o][:, :, cols])
-                nc.vector.quantize_mx(q_codes[o][:, cols].bitcast(FP8X4), q_scale[o][:, cols], q_bf[:].rearrange("p q t -> p (q t)"))
+        q_bf = {}
+
+        def cast(copy, o, c, tag):
+            q_bf[o, c] = sb.tile([P, P, 4], BF16, name="q_bf%d%d" % (o, c), tag=tag, align_bytes=64)
+            interleave(copy, q_bf[o, c][:], q_raw[o][:, :, c * P : (c + 1) * P])
+
+        def quantize(o, c):
+            cols = slice(c * P, (c + 1) * P)
+            nc.vector.quantize_mx(q_codes[o][:, cols].bitcast(FP8X4), q_scale[o][:, cols], q_bf[o, c][:].rearrange("p q t -> p (q t)"))
+
+        cast(nc.scalar.copy, 0, 0, "q_bf00")
+        cast(nc.vector.tensor_copy, 0, 1, "q_bf01")
+        quantize(0, 0)
+        quantize(0, 1)
+        cast(nc.scalar.copy, 1, 0, "q_bf10")
+        cast(nc.vector.tensor_copy, 1, 1, "q_raw0")
+        quantize(1, 0)
+        quantize(1, 1)
+        rk_rows = sb.tile([P, N], F32, name="rk_rows", tag="q_raw1", align_bytes=64)
+        nc.scalar.copy(rk_rows[:], rk_spread[:])
 
         acc = [ps.tile([P, N], F32, name="acc%d" % c) for c in range(2)]
         for o in range(2):
@@ -101,7 +124,7 @@ def tile_attend_cosexp_topk_kernel(tc, qT, k_words, k_scales, rk, rq, offs, out)
                     acc[c][:],
                     lhsT=q_codes[o][:, cols].bitcast(FP8X4),
                     lhsT_scale=q_scale[o][:, cols],
-                    rhs=k_codes[:, o, :].bitcast(FP4X4),
+                    rhs=k_codes[o][:].bitcast(FP4X4),
                     rhs_scale=k_scale[o][:],
                     start=(o == 0),
                     stop=(o == 1),
@@ -111,7 +134,7 @@ def tile_attend_cosexp_topk_kernel(tc, qT, k_words, k_scales, rk, rq, offs, out)
             for h in range(2):
                 slots = slice(h * HALF, (h + 1) * HALF)
                 scaled = sb.tile([P, HALF], F32, name="scaled%d%d" % (c, h))
-                nc.vector.scalar_tensor_tensor(scaled[:], acc[c][:, slots], rq_col[c][:], rk_rows[:, slots], MULT, MULT)
+                nc.vector.scalar_tensor_tensor(scaled[:], acc[c][:, slots], rq_turned[:, P - 2 + c : P - 1 + c], rk_rows[:, slots], MULT, MULT)
                 result = sb.tile([P, HALF], F32, name="result%d%d" % (c, h))
-                nc.scalar.activation(result[:], scaled[:], ACT.Exp, bias=-10.0, scale=10.0)
+                nc.scalar.activation(result[:], scaled[:], ACT.Exp, bias=bias[:])
                 nc.sync.dma_start(out[0, c * P : (c + 1) * P, slots], result[:])

@@ -111,14 +111,16 @@ def tile_attend_cosexp_topk_kernel(tc, qT, k_words, k_scales, rk, rq, offs, out)
         quantize(0, 1)
         cast(nc.scalar.copy, 1, 0, "q_bf10")
         cast(nc.vector.tensor_copy, 1, 1, "q_raw0")
-        quantize(1, 0)
         quantize(1, 1)
-        rk_rows = sb.tile([P, N], F32, name="rk_rows", tag="q_raw1", align_bytes=64)
+        quantize(1, 0)
+        rk_rows = sb.tile([P, N], F32, name="rk_rows")
         nc.scalar.copy(rk_rows[:], rk_spread[:])
+        rq_cols = sb.tile([P, 2], F32, name="rq_cols")
+        nc.scalar.copy(rq_cols[:], rq_turned[:, P - 2 : P])
 
         acc = [ps.tile([P, N], F32, name="acc%d" % c) for c in range(2)]
         for o in range(2):
-            for c in range(2):
+            for c in (o, 1 - o):
                 cols = slice(c * P, (c + 1) * P)
                 nc.tensor.matmul_mx(
                     acc[c][:],
@@ -130,11 +132,11 @@ def tile_attend_cosexp_topk_kernel(tc, qT, k_words, k_scales, rk, rq, offs, out)
                     stop=(o == 1),
                 )
 
-        for c in range(2):
+        for c in (1, 0):
             for h in range(2):
                 slots = slice(h * HALF, (h + 1) * HALF)
                 scaled = sb.tile([P, HALF], F32, name="scaled%d%d" % (c, h))
-                nc.vector.scalar_tensor_tensor(scaled[:], acc[c][:, slots], rq_turned[:, P - 2 + c : P - 1 + c], rk_rows[:, slots], MULT, MULT)
+                nc.vector.tensor_tensor(scaled[:], acc[c][:, slots], rk_rows[:, slots], MULT)
                 result = sb.tile([P, HALF], F32, name="result%d%d" % (c, h))
-                nc.scalar.activation(result[:], scaled[:], ACT.Exp, bias=bias[:])
+                nc.scalar.activation(result[:], scaled[:], ACT.Exp, bias=bias[:], scale=rq_cols[:, c : c + 1])
                 nc.sync.dma_start(out[0, c * P : (c + 1) * P, slots], result[:])

@@ -1,3 +1,4 @@
+import math
 from contextlib import ExitStack
 
 import concourse.mybir as mybir
@@ -18,11 +19,11 @@ ACT = mybir.ActivationFunctionType
 MULT = mybir.AluOpType.mult
 
 P = 128
-HALF = N // 2
-
-
-def interleave(copy, grouped, raw):
-    copy(grouped.rearrange("p (c i) t -> p c t i", i=4), raw.rearrange("p t (c i) -> p c t i", i=4))
+PASSES = D // 512
+TILES = NQ // P
+GAIN = 10.0
+SCALE_ROW0 = 48
+CHUNK = N // 2
 
 
 def tile_attend_cosexp_topk_kernel(tc, qT, k_words, k_scales, rk, rq, offs, out):
@@ -34,109 +35,113 @@ def tile_attend_cosexp_topk_kernel(tc, qT, k_words, k_scales, rk, rq, offs, out)
         offsets = sb.tile([P, N // 16], U16, name="offsets")
         nc.sync.dma_start(offsets[:], offs)
 
-        ident = sb.tile([P, P], F32, name="ident")
+        ident = sb.tile([P, P], F32, name="ident", tag="ident", align_bytes=64)
         make_identity(nc, ident[:])
+        minus_gain = sb.tile([P, 1], F32, name="minus_gain")
+        nc.vector.memset(minus_gain[:], -GAIN)
 
-        bias = sb.tile([P, 1], F32, name="bias")
-        nc.vector.memset(bias[:], -10.0)
-        ten = sb.tile([P, 1], F32, name="ten", tag="q_bf00", align_bytes=64)
-        nc.vector.memset(ten[:], 10.0)
         scale_pool = sb.tile([P, T], U8, name="scale_pool")
-        for lo, hi in ((0, 48), (64, 80), (96, 128)):
+        for lo, hi in ((0, SCALE_ROW0), (64, SCALE_ROW0 + 32), (96, P)):
             nc.vector.memset(scale_pool[lo:hi, :].bitcast(I32), 0)
-        scale_words = k_scales.bitcast(I32).rearrange("o (h e j) t -> e (o h) j t", e=2, j=4)
+        scale_rows = k_scales.bitcast(I32).rearrange("o (h e j) t -> e (o h) j t", e=2, j=4)
         for e in range(2):
-            nc.sync.dma_start(scale_pool[48 + 32 * e : 64 + 32 * e, :].bitcast(I32), scale_words[e])
+            first = SCALE_ROW0 + 32 * e
+            nc.sync.dma_start(scale_pool[first : first + 16, :].bitcast(I32), scale_rows[e])
+
         rk_pool = sb.tile([P, T], F32, name="rk_pool")
         nc.vector.memset(rk_pool[0 : P - 1, :], 0.0)
         nc.scalar.dma_start(rk_pool[P - 1 : P, :], rk[0:1, :])
-        word_pool = sb.tile([P, T], I32, name="word_pool", tag="q_bf01", align_bytes=64)
+
+        word_pool = sb.tile([P, T], I32, name="word_pool", tag="word_pool", align_bytes=64)
         nc.sync.dma_start(word_pool[:], k_words[0].rearrange("p t b -> p (t b)").bitcast(I32))
 
         rq_rows = sb.tile([P, P], F32, name="rq_rows")
-        nc.gpsimd.memset(rq_rows[0 : P - 2, :], 0.0)
-        nc.sync.dma_start(rq_rows[P - 2 : P, :], rq[0].rearrange("(c q) one -> c (q one)", c=2))
+        nc.gpsimd.memset(rq_rows[0 : P - TILES, :], 0.0)
+        nc.sync.dma_start(rq_rows[P - TILES : P, :], rq[0].rearrange("(c q) one -> c (q one)", c=TILES))
 
-        q_rows = qT[0].rearrange("(o p t) q -> o p t q", o=2, t=4)
-        q_raw = [sb.tile([P, 4, NQ], F32, name="q_raw%d" % o, tag="q_raw%d" % o, align_bytes=64) for o in range(2)]
-        for o in range(2):
+        q_rows = qT[0].rearrange("(o p t) q -> o p t q", o=PASSES, t=4)
+        q_raw = [sb.tile([P, 4, NQ], F32, name="q_raw%d" % o, tag="q_raw%d" % o, align_bytes=64) for o in range(PASSES)]
+        for o in range(PASSES):
             nc.sync.dma_start(q_raw[o][:], q_rows[o])
 
-        warm = sb.tile([P, 1], F32, name="warm")
-        nc.scalar.activation(warm[:], bias[:], ACT.Exp)
+        gain = sb.tile([P, 1], F32, name="gain", tag="gain", align_bytes=64)
+        nc.scalar.activation(gain[:], minus_gain[:], ACT.Exp, scale=-math.log(GAIN) / GAIN)
 
         listed_scales = sb.tile([P, N], U8, name="listed_scales")
         nc.vector.tensor_copy(listed_scales[:], scale_pool[:].indirect(offsets[:]))
-        k_scale = [sb.tile([P, N], U8, name="k_scale%d" % o, align_bytes=64) for o in range(2)]
-        for o in range(2):
+        k_scale = [sb.tile([P, N], U8, name="k_scale%d" % o, align_bytes=64) for o in range(PASSES)]
+        for o in range(PASSES):
             for h in range(2):
-                first = 48 + 4 * (2 * o + h)
-                nc.scalar.dma_start(k_scale[o][64 * h : 64 * h + 64, :].bitcast(I32), listed_scales[first : first + 64, :].bitcast(I32))
+                first = SCALE_ROW0 + 4 * (2 * o + h)
+                nc.scalar.dma_start(
+                    k_scale[o][64 * h : 64 * h + 64, :].bitcast(I32), listed_scales[first : first + 64, :].bitcast(I32)
+                )
 
         rk_listed = sb.tile([P, N], F32, name="rk_listed")
         nc.vector.tensor_copy(rk_listed[:], rk_pool[:].indirect(offsets[:]))
-        rk_turned = ps.tile([P, 4, P], F32, name="rk_turned", tag="turned")
-        for c in range(4):
-            nc.tensor.transpose(rk_turned[:, c, :], rk_listed[:, c * P : (c + 1) * P], ident[:])
-        rk_cols = sb.tile([P, 4], F32, name="rk_cols", tag="q_bf10", align_bytes=64)
-        nc.scalar.activation(rk_cols[:], rk_turned[:, :, P - 1], ACT.Copy, scale=ten[:])
+        rk_turned = ps.tile([P, N // P, P], F32, name="rk_turned", tag="turned")
+        for s in range(N // P):
+            nc.tensor.transpose(rk_turned[:, s, :], rk_listed[:, s * P : (s + 1) * P], ident[:])
+        rk_cols = sb.tile([P, N // P], F32, name="rk_cols", tag="rk_cols", align_bytes=64)
+        nc.scalar.activation(rk_cols[:], rk_turned[:, :, P - 1], ACT.Copy, scale=gain[:])
         rk_spread = ps.tile([P, N], F32, name="rk_spread")
-        for c in range(4):
-            nc.tensor.transpose(rk_spread[:, c * P : (c + 1) * P], rk_cols[:, c : c + 1].to_broadcast([P, P]), ident[:])
+        for s in range(N // P):
+            nc.tensor.transpose(rk_spread[:, s * P : (s + 1) * P], rk_cols[:, s : s + 1].to_broadcast([P, P]), ident[:])
 
         rq_turned = ps.tile([P, P], F32, name="rq_turned", tag="turned")
         nc.tensor.transpose(rq_turned[:], rq_rows[:], ident[:])
 
         listed_words = sb.tile([P, N], U32, name="listed_words")
         nc.vector.tensor_copy(listed_words[:], word_pool[:].bitcast(U32).indirect(offsets[:]))
-        k_codes = [sb.tile([P, N], U16, name="k_codes%d" % o, align_bytes=64) for o in range(2)]
-        for o in range(2):
-            nc.vector.tensor_copy(k_codes[o][:], listed_words[:].bitcast(U16)[:, o::2])
+        k_codes = [sb.tile([P, N], U16, name="k_codes%d" % o, align_bytes=64) for o in range(PASSES)]
+        for o in range(PASSES):
+            nc.vector.tensor_copy(k_codes[o][:], listed_words[:].bitcast(U16)[:, o::PASSES])
 
-        q_codes = [sb.tile([P, NQ], U32, name="q_codes%d" % o, align_bytes=64) for o in range(2)]
-        q_scale = [sb.tile([P, NQ], U8, name="q_scale%d" % o, align_bytes=64) for o in range(2)]
-        q_bf = {}
+        q_bf, q_codes, q_scale = {}, {}, {}
 
         def cast(copy, o, c, tag):
             q_bf[o, c] = sb.tile([P, P, 4], BF16, name="q_bf%d%d" % (o, c), tag=tag, align_bytes=64)
-            interleave(copy, q_bf[o, c][:], q_raw[o][:, :, c * P : (c + 1) * P])
+            copy(
+                q_bf[o, c][:].rearrange("p (g i) t -> p g t i", i=4),
+                q_raw[o][:, :, c * P : (c + 1) * P].rearrange("p t (g i) -> p g t i", i=4),
+            )
 
-        def quantize(o, c):
-            cols = slice(c * P, (c + 1) * P)
-            nc.vector.quantize_mx(q_codes[o][:, cols].bitcast(FP8X4), q_scale[o][:, cols], q_bf[o, c][:].rearrange("p q t -> p (q t)"))
+        def quantize(o, c, tag):
+            q_codes[o, c] = sb.tile([P, P], U32, name="q_codes%d%d" % (o, c), tag=tag, align_bytes=64)
+            q_scale[o, c] = sb.tile([P, P], U8, name="q_scale%d%d" % (o, c), align_bytes=64)
+            nc.vector.quantize_mx(q_codes[o, c][:].bitcast(FP8X4), q_scale[o, c][:], q_bf[o, c][:].rearrange("p q t -> p (q t)"))
 
-        cast(nc.scalar.copy, 0, 0, "q_bf00")
-        cast(nc.vector.tensor_copy, 0, 1, "q_bf01")
-        quantize(0, 0)
-        quantize(0, 1)
-        cast(nc.scalar.copy, 1, 0, "q_bf10")
+        cast(nc.scalar.copy, 0, 0, "gain")
+        cast(nc.vector.tensor_copy, 0, 1, "word_pool")
+        quantize(0, 0, "q_codes00")
+        quantize(0, 1, "ident")
+        cast(nc.scalar.copy, 1, 0, "rk_cols")
         cast(nc.vector.tensor_copy, 1, 1, "q_raw0")
-        quantize(1, 1)
-        quantize(1, 0)
+        quantize(1, 1, "q_codes11")
+        quantize(1, 0, "q_codes10")
+
         rk_rows = sb.tile([P, N], F32, name="rk_rows")
         nc.scalar.copy(rk_rows[:], rk_spread[:])
-        rq_cols = sb.tile([P, 2], F32, name="rq_cols")
-        nc.scalar.copy(rq_cols[:], rq_turned[:, P - 2 : P])
+        rq_cols = sb.tile([P, TILES], F32, name="rq_cols")
+        nc.scalar.copy(rq_cols[:], rq_turned[:, P - TILES : P])
 
-        acc = [ps.tile([P, N], F32, name="acc%d" % c) for c in range(2)]
-        for o in range(2):
-            for c in (o, 1 - o):
-                cols = slice(c * P, (c + 1) * P)
-                nc.tensor.matmul_mx(
-                    acc[c][:],
-                    lhsT=q_codes[o][:, cols].bitcast(FP8X4),
-                    lhsT_scale=q_scale[o][:, cols],
-                    rhs=k_codes[o][:].bitcast(FP4X4),
-                    rhs_scale=k_scale[o][:],
-                    start=(o == 0),
-                    stop=(o == 1),
-                )
+        scores = [ps.tile([P, N], F32, name="scores%d" % c) for c in range(TILES)]
+        for o, c in ((0, 0), (0, 1), (1, 1), (1, 0)):
+            nc.tensor.matmul_mx(
+                scores[c][:],
+                lhsT=q_codes[o, c][:].bitcast(FP8X4),
+                lhsT_scale=q_scale[o, c][:],
+                rhs=k_codes[o][:].bitcast(FP4X4),
+                rhs_scale=k_scale[o][:],
+                start=(o == 0),
+                stop=(o == PASSES - 1),
+            )
 
         for c in (1, 0):
-            for h in range(2):
-                slots = slice(h * HALF, (h + 1) * HALF)
-                scaled = sb.tile([P, HALF], F32, name="scaled%d%d" % (c, h))
-                nc.vector.tensor_tensor(scaled[:], acc[c][:, slots], rk_rows[:, slots], MULT)
-                result = sb.tile([P, HALF], F32, name="result%d%d" % (c, h))
-                nc.scalar.activation(result[:], scaled[:], ACT.Exp, bias=bias[:], scale=rq_cols[:, c : c + 1])
+            for u in range(N // CHUNK):
+                slots = slice(u * CHUNK, (u + 1) * CHUNK)
+                scaled = sb.tile([P, CHUNK], F32, name="scaled%d%d" % (c, u))
+                nc.vector.tensor_tensor(scaled[:], scores[c][:, slots], rk_rows[:, slots], MULT)
+                result = sb.tile([P, CHUNK], F32, name="result%d%d" % (c, u))
+                nc.scalar.activation(result[:], scaled[:], ACT.Exp, bias=minus_gain[:], scale=rq_cols[:, c : c + 1])
                 nc.sync.dma_start(out[0, c * P : (c + 1) * P, slots], result[:])

@@ -22,7 +22,7 @@ P = 128
 PASSES = D // 512
 TILES = NQ // P
 GAIN = 10.0
-SCALE_ROW0 = 48
+SCALE_ROW0 = 96
 CHUNK = N // 2
 
 
@@ -41,12 +41,8 @@ def tile_attend_cosexp_topk_kernel(tc, qT, k_words, k_scales, rk, rq, offs, out)
         nc.vector.memset(minus_gain[:], -GAIN)
 
         scale_pool = sb.tile([P, T], U8, name="scale_pool")
-        for lo, hi in ((0, SCALE_ROW0), (64, SCALE_ROW0 + 32), (96, P)):
-            nc.vector.memset(scale_pool[lo:hi, :].bitcast(I32), 0)
-        scale_rows = k_scales.bitcast(I32).rearrange("o (h e j) t -> e (o h) j t", e=2, j=4)
-        for e in range(2):
-            first = SCALE_ROW0 + 32 * e
-            nc.sync.dma_start(scale_pool[first : first + 16, :].bitcast(I32), scale_rows[e])
+        nc.sync.dma_start(scale_pool[SCALE_ROW0:P, :].bitcast(I32), k_scales.bitcast(I32).rearrange("o f t -> f o t"))
+        nc.vector.memset(scale_pool[0:SCALE_ROW0, :].bitcast(I32), 0)
 
         rk_pool = sb.tile([P, T], F32, name="rk_pool")
         nc.vector.memset(rk_pool[0 : P - 1, :], 0.0)
@@ -69,13 +65,13 @@ def tile_attend_cosexp_topk_kernel(tc, qT, k_words, k_scales, rk, rq, offs, out)
 
         listed_scales = sb.tile([P, N], U8, name="listed_scales")
         nc.vector.tensor_copy(listed_scales[:], scale_pool[:].indirect(offsets[:]))
-        k_scale = [sb.tile([P, N], U8, name="k_scale%d" % o, align_bytes=64) for o in range(PASSES)]
-        for o in range(PASSES):
-            for h in range(2):
-                first = SCALE_ROW0 + 4 * (2 * o + h)
-                nc.scalar.dma_start(
-                    k_scale[o][64 * h : 64 * h + 64, :].bitcast(I32), listed_scales[first : first + 64, :].bitcast(I32)
-                )
+        k_scale = sb.tile([P, PASSES, N], U8, name="k_scale", align_bytes=64)
+        nc.gpsimd.memset(k_scale[:].rearrange("p o n -> p (o n)").bitcast(I32), 0)
+        for u in range(4):
+            first = SCALE_ROW0 + 8 * u
+            nc.scalar.dma_start(
+                k_scale[32 * u : 32 * u + 4, :, :].bitcast(I32), listed_scales[first : first + 8, :].bitcast(I32)
+            )
 
         rk_listed = sb.tile([P, N], F32, name="rk_listed")
         nc.vector.tensor_copy(rk_listed[:], rk_pool[:].indirect(offsets[:]))
@@ -91,7 +87,7 @@ def tile_attend_cosexp_topk_kernel(tc, qT, k_words, k_scales, rk, rq, offs, out)
         rq_turned = ps.tile([P, P], F32, name="rq_turned", tag="turned")
         nc.tensor.transpose(rq_turned[:], rq_rows[:], ident[:])
 
-        listed_words = sb.tile([P, N], U32, name="listed_words")
+        listed_words = sb.tile([P, N], U32, name="listed_words", tag="listed_words", align_bytes=64)
         nc.vector.tensor_copy(listed_words[:], word_pool[:].bitcast(U32).indirect(offsets[:]))
         k_codes = [sb.tile([P, N], U16, name="k_codes%d" % o, align_bytes=64) for o in range(PASSES)]
         for o in range(PASSES):
@@ -112,13 +108,13 @@ def tile_attend_cosexp_topk_kernel(tc, qT, k_words, k_scales, rk, rq, offs, out)
             nc.vector.quantize_mx(q_codes[o, c][:].bitcast(FP8X4), q_scale[o, c][:], q_bf[o, c][:].rearrange("p q t -> p (q t)"))
 
         cast(nc.scalar.copy, 0, 0, "gain")
-        cast(nc.vector.tensor_copy, 0, 1, "word_pool")
+        cast(nc.scalar.copy, 0, 1, "q_bf01")
         quantize(0, 0, "q_codes00")
         quantize(0, 1, "ident")
         cast(nc.scalar.copy, 1, 0, "rk_cols")
-        cast(nc.vector.tensor_copy, 1, 1, "q_raw0")
-        quantize(1, 1, "q_codes11")
+        cast(nc.vector.tensor_copy, 1, 1, "listed_words")
         quantize(1, 0, "q_codes10")
+        quantize(1, 1, "q_codes11")
 
         rk_rows = sb.tile([P, N], F32, name="rk_rows")
         nc.scalar.copy(rk_rows[:], rk_spread[:])
@@ -126,18 +122,18 @@ def tile_attend_cosexp_topk_kernel(tc, qT, k_words, k_scales, rk, rq, offs, out)
         nc.scalar.copy(rq_cols[:], rq_turned[:, P - TILES : P])
 
         scores = [ps.tile([P, N], F32, name="scores%d" % c) for c in range(TILES)]
-        for o, c in ((0, 0), (0, 1), (1, 1), (1, 0)):
+        for o, c in ((0, 0), (0, 1), (1, 0), (1, 1)):
             nc.tensor.matmul_mx(
                 scores[c][:],
                 lhsT=q_codes[o, c][:].bitcast(FP8X4),
                 lhsT_scale=q_scale[o, c][:],
                 rhs=k_codes[o][:].bitcast(FP4X4),
-                rhs_scale=k_scale[o][:],
+                rhs_scale=k_scale[:, o, :],
                 start=(o == 0),
                 stop=(o == PASSES - 1),
             )
 
-        for c in (1, 0):
+        for c in range(TILES):
             for u in range(N // CHUNK):
                 slots = slice(u * CHUNK, (u + 1) * CHUNK)
                 scaled = sb.tile([P, CHUNK], F32, name="scaled%d%d" % (c, u))

@@ -23,6 +23,7 @@ PASSES = D // 512
 TILES = NQ // P
 GAIN = 10.0
 SCALE_ROW0 = 96
+HALF = N // 2
 CHUNK = N // 2
 
 
@@ -35,25 +36,25 @@ def tile_attend_cosexp_topk_kernel(tc, qT, k_words, k_scales, rk, rq, offs, out)
         offsets = sb.tile([P, N // 16], U16, name="offsets")
         nc.sync.dma_start(offsets[:], offs)
 
+        rk_pool = sb.tile([P, T], F32, name="rk_pool")
+        nc.gpsimd.memset(rk_pool[0 : P - 1, :], 0.0)
+        nc.scalar.dma_start(rk_pool[P - 1 : P, :], rk[0:1, :])
+
         ident = sb.tile([P, P], F32, name="ident", tag="ident", align_bytes=64)
         make_identity(nc, ident[:])
         minus_gain = sb.tile([P, 1], F32, name="minus_gain")
         nc.vector.memset(minus_gain[:], -GAIN)
 
-        scale_pool = sb.tile([P, T], U8, name="scale_pool")
-        nc.sync.dma_start(scale_pool[SCALE_ROW0:P, :].bitcast(I32), k_scales.bitcast(I32).rearrange("o f t -> f o t"))
+        scale_pool = sb.tile([P, T + 4], U8, name="scale_pool")
+        nc.sync.dma_start(scale_pool[SCALE_ROW0:P, 0:T].bitcast(I32), k_scales.bitcast(I32).rearrange("o f t -> f o t"))
         nc.vector.memset(scale_pool[0:SCALE_ROW0, :].bitcast(I32), 0)
 
-        rk_pool = sb.tile([P, T], F32, name="rk_pool")
-        nc.vector.memset(rk_pool[0 : P - 1, :], 0.0)
-        nc.scalar.dma_start(rk_pool[P - 1 : P, :], rk[0:1, :])
+        rq_rows = sb.tile([P, P + 1], F32, name="rq_rows")
+        nc.vector.memset(rq_rows[0 : P - TILES, :], 0.0)
+        nc.sync.dma_start(rq_rows[P - TILES : P, 0:P], rq[0].rearrange("(c q) one -> c (q one)", c=TILES))
 
         word_pool = sb.tile([P, T], I32, name="word_pool", tag="word_pool", align_bytes=64)
         nc.sync.dma_start(word_pool[:], k_words[0].rearrange("p t b -> p (t b)").bitcast(I32))
-
-        rq_rows = sb.tile([P, P], F32, name="rq_rows")
-        nc.gpsimd.memset(rq_rows[0 : P - TILES, :], 0.0)
-        nc.sync.dma_start(rq_rows[P - TILES : P, :], rq[0].rearrange("(c q) one -> c (q one)", c=TILES))
 
         q_rows = qT[0].rearrange("(o p t) q -> o p t q", o=PASSES, t=4)
         q_raw = [sb.tile([P, 4, NQ], F32, name="q_raw%d" % o, tag="q_raw%d" % o, align_bytes=64) for o in range(PASSES)]
@@ -63,29 +64,34 @@ def tile_attend_cosexp_topk_kernel(tc, qT, k_words, k_scales, rk, rq, offs, out)
         gain = sb.tile([P, 1], F32, name="gain", tag="gain", align_bytes=64)
         nc.scalar.activation(gain[:], minus_gain[:], ACT.Exp, scale=-math.log(GAIN) / GAIN)
 
+        k_scale = sb.tile([P, PASSES * N + 4], U8, name="k_scale", align_bytes=64)
+        nc.vector.memset(k_scale[:].bitcast(I32), 0)
         listed_scales = sb.tile([P, N], U8, name="listed_scales")
-        nc.vector.tensor_copy(listed_scales[:], scale_pool[:].indirect(offsets[:]))
-        k_scale = sb.tile([P, PASSES, N], U8, name="k_scale", align_bytes=64)
-        nc.gpsimd.memset(k_scale[:].rearrange("p o n -> p (o n)").bitcast(I32), 0)
+        nc.vector.tensor_copy(listed_scales[:], scale_pool[:, 0:T].indirect(offsets[:]))
         for u in range(4):
             first = SCALE_ROW0 + 8 * u
             nc.scalar.dma_start(
-                k_scale[32 * u : 32 * u + 4, :, :].bitcast(I32), listed_scales[first : first + 8, :].bitcast(I32)
+                k_scale[32 * u : 32 * u + 4, 0 : PASSES * N].bitcast(I32), listed_scales[first : first + 8, :].bitcast(I32)
             )
 
-        rk_listed = sb.tile([P, N], F32, name="rk_listed")
-        nc.vector.tensor_copy(rk_listed[:], rk_pool[:].indirect(offsets[:]))
-        rk_turned = ps.tile([P, N // P, P], F32, name="rk_turned", tag="turned")
-        for s in range(N // P):
-            nc.tensor.transpose(rk_turned[:, s, :], rk_listed[:, s * P : (s + 1) * P], ident[:])
-        rk_cols = sb.tile([P, N // P], F32, name="rk_cols", tag="rk_cols", align_bytes=64)
-        nc.scalar.activation(rk_cols[:], rk_turned[:, :, P - 1], ACT.Copy, scale=gain[:])
-        rk_spread = ps.tile([P, N], F32, name="rk_spread")
-        for s in range(N // P):
-            nc.tensor.transpose(rk_spread[:, s * P : (s + 1) * P], rk_cols[:, s : s + 1].to_broadcast([P, P]), ident[:])
+        rq_turned = ps.tile([P, P], F32, name="rq_turned", tag="bank1")
+        nc.tensor.transpose(rq_turned[:], rq_rows[:, 0:P], ident[:])
+        rq_cols = sb.tile([P, TILES], F32, name="rq_cols")
+        nc.scalar.copy(rq_cols[:], rq_turned[:, P - TILES : P])
 
-        rq_turned = ps.tile([P, P], F32, name="rq_turned", tag="turned")
-        nc.tensor.transpose(rq_turned[:], rq_rows[:], ident[:])
+        rk_spread = ps.tile([P, N], F32, name="rk_spread")
+        rk_cols = []
+        for h in range(2):
+            rk_listed = sb.tile([P, HALF], F32, name="rk_listed%d" % h, tag="rk_listed%d" % h, align_bytes=64)
+            nc.vector.tensor_copy(rk_listed[:], rk_pool[:].indirect(offsets[:, h * HALF // 16 : (h + 1) * HALF // 16]))
+            rk_turned = ps.tile([P, HALF // P, P], F32, name="rk_turned%d" % h, tag="bank%d" % (2 * h))
+            for s in range(HALF // P):
+                nc.tensor.transpose(rk_turned[:, s, :], rk_listed[:, s * P : (s + 1) * P], ident[:])
+            rk_cols.append(sb.tile([P, HALF // P], F32, name="rk_cols%d" % h, tag="rk_cols%d" % h, align_bytes=64))
+            nc.scalar.activation(rk_cols[h][:], rk_turned[:, :, P - 1], ACT.Copy, scale=gain[:])
+        for s in range(N // P):
+            column = rk_cols[s * P // HALF][:, s % (HALF // P) : s % (HALF // P) + 1]
+            nc.tensor.transpose(rk_spread[:, s * P : (s + 1) * P], column.to_broadcast([P, P]), ident[:])
 
         listed_words = sb.tile([P, N], U32, name="listed_words", tag="listed_words", align_bytes=64)
         nc.vector.tensor_copy(listed_words[:], word_pool[:].bitcast(U32).indirect(offsets[:]))
@@ -107,33 +113,31 @@ def tile_attend_cosexp_topk_kernel(tc, qT, k_words, k_scales, rk, rq, offs, out)
             q_scale[o, c] = sb.tile([P, P], U8, name="q_scale%d%d" % (o, c), align_bytes=64)
             nc.vector.quantize_mx(q_codes[o, c][:].bitcast(FP8X4), q_scale[o, c][:], q_bf[o, c][:].rearrange("p q t -> p (q t)"))
 
-        cast(nc.scalar.copy, 0, 0, "gain")
-        cast(nc.scalar.copy, 0, 1, "q_bf01")
+        cast(nc.scalar.copy, 0, 0, "rk_listed1")
+        cast(nc.scalar.copy, 0, 1, "gain")
         quantize(0, 0, "q_codes00")
-        quantize(0, 1, "ident")
-        cast(nc.scalar.copy, 1, 0, "rk_cols")
-        cast(nc.vector.tensor_copy, 1, 1, "listed_words")
-        quantize(1, 0, "q_codes10")
+        cast(nc.scalar.copy, 1, 0, "rk_cols1")
+        cast(nc.vector.tensor_copy, 1, 1, "rk_listed1")
+        quantize(0, 1, "q_codes01")
         quantize(1, 1, "q_codes11")
+        quantize(1, 0, "q_codes10")
 
-        rk_rows = sb.tile([P, N], F32, name="rk_rows")
+        rk_rows = sb.tile([P, N], F32, name="rk_rows", tag="q_raw1", align_bytes=64)
         nc.scalar.copy(rk_rows[:], rk_spread[:])
-        rq_cols = sb.tile([P, TILES], F32, name="rq_cols")
-        nc.scalar.copy(rq_cols[:], rq_turned[:, P - TILES : P])
 
-        scores = [ps.tile([P, N], F32, name="scores%d" % c) for c in range(TILES)]
-        for o, c in ((0, 0), (0, 1), (1, 0), (1, 1)):
+        scores = [ps.tile([P, N], F32, name="scores%d" % c, tag="bank%d" % (2 - c)) for c in range(TILES)]
+        for o, c in ((0, 0), (0, 1), (1, 1), (1, 0)):
             nc.tensor.matmul_mx(
                 scores[c][:],
                 lhsT=q_codes[o, c][:].bitcast(FP8X4),
                 lhsT_scale=q_scale[o, c][:],
                 rhs=k_codes[o][:].bitcast(FP4X4),
-                rhs_scale=k_scale[:, o, :],
+                rhs_scale=k_scale[:, o * N : (o + 1) * N],
                 start=(o == 0),
                 stop=(o == PASSES - 1),
             )
 
-        for c in range(TILES):
+        for c in (1, 0):
             for u in range(N // CHUNK):
                 slots = slice(u * CHUNK, (u + 1) * CHUNK)
                 scaled = sb.tile([P, CHUNK], F32, name="scaled%d%d" % (c, u))

@@ -94,10 +94,17 @@ def tile_attend_cosexp_topk_kernel(tc, qT, k_words, k_scales, rk, rq, offs, out)
             nc.tensor.transpose(rk_spread[:, s * P : (s + 1) * P], column.to_broadcast([P, P]), ident[:])
 
         listed_words = sb.tile([P, N], U32, name="listed_words", tag="listed_words", align_bytes=64)
-        nc.vector.tensor_copy(listed_words[:], word_pool[:].bitcast(U32).indirect(offsets[:]))
-        k_codes = [sb.tile([P, N], U16, name="k_codes%d" % o, align_bytes=64) for o in range(PASSES)]
-        for o in range(PASSES):
-            nc.vector.tensor_copy(k_codes[o][:], listed_words[:].bitcast(U16)[:, o::PASSES])
+        for h in range(2):
+            nc.vector.tensor_copy(
+                listed_words[:, h * HALF : (h + 1) * HALF],
+                word_pool[:].bitcast(U32).indirect(offsets[:, h * HALF // 16 : (h + 1) * HALF // 16]),
+            )
+        k_codes = sb.tile([P, PASSES, N], U16, name="k_codes", align_bytes=64)
+        for h in range(2):
+            nc.vector.tensor_copy(
+                k_codes[:, :, h * HALF : (h + 1) * HALF],
+                listed_words[:, h * HALF : (h + 1) * HALF].bitcast(U16).rearrange("p (n o) -> p o n", o=PASSES),
+            )
 
         q_bf, q_codes, q_scale = {}, {}, {}
 
@@ -123,25 +130,41 @@ def tile_attend_cosexp_topk_kernel(tc, qT, k_words, k_scales, rk, rq, offs, out)
         quantize(1, 0, "q_codes10")
 
         rk_rows = sb.tile([P, N], F32, name="rk_rows", tag="q_raw1", align_bytes=64)
-        nc.scalar.copy(rk_rows[:], rk_spread[:])
+        for h in range(2):
+            nc.scalar.copy(rk_rows[:, h * HALF : (h + 1) * HALF], rk_spread[:, h * HALF : (h + 1) * HALF])
 
-        scores = [ps.tile([P, N], F32, name="scores%d" % c, tag="bank%d" % (2 - c)) for c in range(TILES)]
-        for o, c in ((0, 0), (0, 1), (1, 1), (1, 0)):
+        scores = {}
+        for u in range(N // CHUNK):
+            scores[1, u] = ps.tile([P, CHUNK], F32, name="scores1%d" % u, tag="bank%d" % u)
+        whole = ps.tile([P, N], F32, name="scores0", tag="bank2")
+        for u in range(N // CHUNK):
+            scores[0, u] = whole[:, u * CHUNK : (u + 1) * CHUNK]
+
+        def matmul(target, o, c, slots, start, stop):
             nc.tensor.matmul_mx(
-                scores[c][:],
+                target,
                 lhsT=q_codes[o, c][:].bitcast(FP8X4),
                 lhsT_scale=q_scale[o, c][:],
-                rhs=k_codes[o][:].bitcast(FP4X4),
-                rhs_scale=k_scale[:, o * N : (o + 1) * N],
-                start=(o == 0),
-                stop=(o == PASSES - 1),
+                rhs=k_codes[:, o, slots].bitcast(FP4X4),
+                rhs_scale=k_scale[:, o * N + slots.start : o * N + slots.stop],
+                start=start,
+                stop=stop,
             )
+
+        for o, c in ((0, 0), (0, 1), (1, 1), (1, 0)):
+            if c == 0:
+                matmul(whole[:], o, c, slice(0, N), o == 0, o == PASSES - 1)
+                continue
+            for s in range(N // P):
+                u, j = divmod(s, CHUNK // P)
+                first, last = (o, j) == (0, 0), (o, j) == (PASSES - 1, CHUNK // P - 1)
+                matmul(scores[1, u][:, j * P : (j + 1) * P], o, c, slice(s * P, (s + 1) * P), first, last)
 
         for c in (1, 0):
             for u in range(N // CHUNK):
                 slots = slice(u * CHUNK, (u + 1) * CHUNK)
                 scaled = sb.tile([P, CHUNK], F32, name="scaled%d%d" % (c, u))
-                nc.vector.tensor_tensor(scaled[:], scores[c][:, slots], rk_rows[:, slots], MULT)
+                nc.vector.tensor_tensor(scaled[:], scores[c, u][:], rk_rows[:, slots], MULT)
                 result = sb.tile([P, CHUNK], F32, name="result%d%d" % (c, u))
                 nc.scalar.activation(result[:], scaled[:], ACT.Exp, bias=minus_gain[:], scale=rq_cols[:, c : c + 1])
                 nc.sync.dma_start(out[0, c * P : (c + 1) * P, slots], result[:])

@@ -38,7 +38,6 @@ def tile_attend_cosexp_topk_kernel(tc, qT, k_words, k_scales, rk, rq, offs, out)
 
         rk_pool = sb.tile([P, T], F32, name="rk_pool")
         nc.gpsimd.memset(rk_pool[0 : P - 1, :], 0.0)
-        nc.scalar.dma_start(rk_pool[P - 1 : P, :], rk[0:1, :])
 
         ident = sb.tile([P, P], F32, name="ident", tag="ident", align_bytes=64)
         make_identity(nc, ident[:])
@@ -49,9 +48,11 @@ def tile_attend_cosexp_topk_kernel(tc, qT, k_words, k_scales, rk, rq, offs, out)
         nc.sync.dma_start(scale_pool[SCALE_ROW0:P, 0:T].bitcast(I32), k_scales.bitcast(I32).rearrange("o f t -> f o t"))
         nc.vector.memset(scale_pool[0:SCALE_ROW0, :].bitcast(I32), 0)
 
+        nc.sync.dma_start(rk_pool[P - 1 : P, :], rk[0:1, :])
+
         rq_rows = sb.tile([P, P + 1], F32, name="rq_rows")
         nc.vector.memset(rq_rows[0 : P - TILES, :], 0.0)
-        nc.sync.dma_start(rq_rows[P - TILES : P, 0:P], rq[0].rearrange("(c q) one -> c (q one)", c=TILES))
+        nc.scalar.dma_start(rq_rows[P - TILES : P, 0:P], rq[0].rearrange("(c q) one -> c (q one)", c=TILES))
 
         word_pool = sb.tile([P, T], I32, name="word_pool", tag="word_pool", align_bytes=64)
         nc.sync.dma_start(word_pool[:], k_words[0].rearrange("p t b -> p (t b)").bitcast(I32))
@@ -79,7 +80,7 @@ def tile_attend_cosexp_topk_kernel(tc, qT, k_words, k_scales, rk, rq, offs, out)
         rq_cols = sb.tile([P, TILES], F32, name="rq_cols")
         nc.scalar.copy(rq_cols[:], rq_turned[:, P - TILES : P])
 
-        rk_spread = ps.tile([P, N], F32, name="rk_spread")
+        rk_spread = [ps.tile([P, HALF], F32, name="rk_spread%d" % h) for h in range(2)]
         rk_cols = []
         for h in range(2):
             rk_listed = sb.tile([P, HALF], F32, name="rk_listed%d" % h, tag="rk_listed%d" % h, align_bytes=64)
@@ -91,7 +92,7 @@ def tile_attend_cosexp_topk_kernel(tc, qT, k_words, k_scales, rk, rq, offs, out)
             nc.scalar.activation(rk_cols[h][:], rk_turned[:, :, P - 1], ACT.Copy, scale=gain[:])
         for s in range(N // P):
             column = rk_cols[s * P // HALF][:, s % (HALF // P) : s % (HALF // P) + 1]
-            nc.tensor.transpose(rk_spread[:, s * P : (s + 1) * P], column.to_broadcast([P, P]), ident[:])
+            nc.tensor.transpose(rk_spread[s * P // HALF][:, s * P % HALF : s * P % HALF + P], column.to_broadcast([P, P]), ident[:])
 
         listed_words = sb.tile([P, N], U32, name="listed_words", tag="listed_words", align_bytes=64)
         for h in range(2):
@@ -105,6 +106,12 @@ def tile_attend_cosexp_topk_kernel(tc, qT, k_words, k_scales, rk, rq, offs, out)
                 k_codes[:, :, h * HALF : (h + 1) * HALF],
                 listed_words[:, h * HALF : (h + 1) * HALF].bitcast(U16).rearrange("p (n o) -> p o n", o=PASSES),
             )
+
+        rk_rows = {}
+
+        def copy_rk(h, tag):
+            rk_rows[h] = sb.tile([P, HALF], F32, name="rk_rows%d" % h, tag=tag, align_bytes=64)
+            nc.scalar.copy(rk_rows[h][:], rk_spread[h][:])
 
         q_bf, q_codes, q_scale = {}, {}, {}
 
@@ -120,18 +127,17 @@ def tile_attend_cosexp_topk_kernel(tc, qT, k_words, k_scales, rk, rq, offs, out)
             q_scale[o, c] = sb.tile([P, P], U8, name="q_scale%d%d" % (o, c), align_bytes=64)
             nc.vector.quantize_mx(q_codes[o, c][:].bitcast(FP8X4), q_scale[o, c][:], q_bf[o, c][:].rearrange("p q t -> p (q t)"))
 
-        cast(nc.scalar.copy, 0, 0, "rk_listed1")
-        cast(nc.scalar.copy, 0, 1, "gain")
+        cast(nc.scalar.copy, 0, 0, "rk_listed0")
+        copy_rk(0, "gain")
+        cast(nc.scalar.copy, 0, 1, "rk_listed1")
         quantize(0, 0, "q_codes00")
         cast(nc.scalar.copy, 1, 0, "rk_cols1")
-        cast(nc.vector.tensor_copy, 1, 1, "rk_listed1")
+        cast(nc.vector.tensor_copy, 1, 1, "rk_listed0")
         quantize(0, 1, "q_codes01")
         quantize(1, 1, "q_codes11")
         quantize(1, 0, "q_codes10")
 
-        rk_rows = sb.tile([P, N], F32, name="rk_rows", tag="q_raw1", align_bytes=64)
-        for h in range(2):
-            nc.scalar.copy(rk_rows[:, h * HALF : (h + 1) * HALF], rk_spread[:, h * HALF : (h + 1) * HALF])
+        copy_rk(1, "q_raw1")
 
         scores = {}
         for u in range(N // CHUNK):
@@ -164,7 +170,7 @@ def tile_attend_cosexp_topk_kernel(tc, qT, k_words, k_scales, rk, rq, offs, out)
             for u in range(N // CHUNK):
                 slots = slice(u * CHUNK, (u + 1) * CHUNK)
                 scaled = sb.tile([P, CHUNK], F32, name="scaled%d%d" % (c, u))
-                nc.vector.tensor_tensor(scaled[:], scores[c, u][:], rk_rows[:, slots], MULT)
+                nc.vector.tensor_tensor(scaled[:], scores[c, u][:], rk_rows[u][:], MULT)
                 result = sb.tile([P, CHUNK], F32, name="result%d%d" % (c, u))
                 nc.scalar.activation(result[:], scaled[:], ACT.Exp, bias=minus_gain[:], scale=rq_cols[:, c : c + 1])
                 nc.sync.dma_start(out[0, c * P : (c + 1) * P, slots], result[:])

@@ -140,11 +140,8 @@ def tile_attend_cosexp_topk_kernel(tc, qT, k_words, k_scales, rk, rq, offs, out)
         copy_rk(1, "q_raw1")
 
         scores = {}
-        for u in range(N // CHUNK):
-            scores[1, u] = ps.tile([P, CHUNK], F32, name="scores1%d" % u, tag="bank%d" % u)
-        whole = ps.tile([P, N], F32, name="scores0", tag="bank2")
-        for u in range(N // CHUNK):
-            scores[0, u] = whole[:, u * CHUNK : (u + 1) * CHUNK]
+        for c, u, tag in ((0, 0, "bank2"), (0, 1, "bank3"), (1, 0, "bank0"), (1, 1, "bank1")):
+            scores[c, u] = ps.tile([P, CHUNK], F32, name="scores%d%d" % (c, u), tag=tag)
 
         def matmul(target, o, c, slots, start, stop):
             nc.tensor.matmul_mx(
@@ -158,13 +155,10 @@ def tile_attend_cosexp_topk_kernel(tc, qT, k_words, k_scales, rk, rq, offs, out)
             )
 
         for o, c in ((0, 0), (0, 1), (1, 1), (1, 0)):
-            if c == 0:
-                matmul(whole[:], o, c, slice(0, N), o == 0, o == PASSES - 1)
-                continue
             for s in range(N // P):
                 u, j = divmod(s, CHUNK // P)
                 first, last = (o, j) == (0, 0), (o, j) == (PASSES - 1, CHUNK // P - 1)
-                matmul(scores[1, u][:, j * P : (j + 1) * P], o, c, slice(s * P, (s + 1) * P), first, last)
+                matmul(scores[c, u][:, j * P : (j + 1) * P], o, c, slice(s * P, (s + 1) * P), first, last)
 
         for c in (1, 0):
             for u in range(N // CHUNK):

@@ -58,9 +58,14 @@ def tile_attend_cosexp_topk_kernel(tc, qT, k_words, k_scales, rk, rq, offs, out)
         nc.sync.dma_start(word_pool[:], k_words[0].rearrange("p t b -> p (t b)").bitcast(I32))
 
         q_rows = qT[0].rearrange("(o p t) q -> o p t q", o=PASSES, t=4)
-        q_raw = [sb.tile([P, 4, NQ], F32, name="q_raw%d" % o, tag="q_raw%d" % o, align_bytes=64) for o in range(PASSES)]
-        for o in range(PASSES):
-            nc.sync.dma_start(q_raw[o][:], q_rows[o])
+        q_raw = {}
+        for c in range(TILES):
+            q_raw[0, c] = sb.tile([P, 4, P], F32, name="q_raw0%d" % c, tag="q_raw0%d" % c, align_bytes=64)
+            nc.sync.dma_start(q_raw[0, c][:], q_rows[0][:, :, c * P : (c + 1) * P])
+        q_raw1 = sb.tile([P, 4, NQ], F32, name="q_raw1", tag="q_raw1", align_bytes=64)
+        nc.sync.dma_start(q_raw1[:], q_rows[1])
+        for c in range(TILES):
+            q_raw[1, c] = q_raw1[:, :, c * P : (c + 1) * P]
 
         gain = sb.tile([P, 1], F32, name="gain", tag="gain", align_bytes=64)
         nc.scalar.activation(gain[:], minus_gain[:], ACT.Exp, scale=-math.log(GAIN) / GAIN)
@@ -100,12 +105,13 @@ def tile_attend_cosexp_topk_kernel(tc, qT, k_words, k_scales, rk, rq, offs, out)
                 listed_words[:, h * HALF : (h + 1) * HALF],
                 word_pool[:].bitcast(U32).indirect(offsets[:, h * HALF // 16 : (h + 1) * HALF // 16]),
             )
-        k_codes = sb.tile([P, PASSES, N], U16, name="k_codes", align_bytes=64)
-        for h in range(2):
-            nc.vector.tensor_copy(
-                k_codes[:, :, h * HALF : (h + 1) * HALF],
-                listed_words[:, h * HALF : (h + 1) * HALF].bitcast(U16).rearrange("p (n o) -> p o n", o=PASSES),
-            )
+        k_codes = {}
+
+        def part(o, tag):
+            k_codes[o] = sb.tile([P, N], U16, name="k_codes%d" % o, tag=tag, align_bytes=64)
+            nc.vector.tensor_copy(k_codes[o][:], listed_words[:].bitcast(U16).rearrange("p (n o) -> p o n", o=PASSES)[:, o, :])
+
+        part(0, "k_codes0")
 
         rk_rows = {}
 
@@ -119,7 +125,7 @@ def tile_attend_cosexp_topk_kernel(tc, qT, k_words, k_scales, rk, rq, offs, out)
             q_bf[o, c] = sb.tile([P, P, 4], BF16, name="q_bf%d%d" % (o, c), tag=tag, align_bytes=64)
             copy(
                 q_bf[o, c][:].rearrange("p (g i) t -> p g t i", i=4),
-                q_raw[o][:, :, c * P : (c + 1) * P].rearrange("p t (g i) -> p g t i", i=4),
+                q_raw[o, c][:].rearrange("p t (g i) -> p g t i", i=4),
             )
 
         def quantize(o, c, tag):
@@ -128,12 +134,13 @@ def tile_attend_cosexp_topk_kernel(tc, qT, k_words, k_scales, rk, rq, offs, out)
             nc.vector.quantize_mx(q_codes[o, c][:].bitcast(FP8X4), q_scale[o, c][:], q_bf[o, c][:].rearrange("p q t -> p (q t)"))
 
         cast(nc.scalar.copy, 0, 0, "rk_listed0")
-        copy_rk(0, "gain")
         cast(nc.scalar.copy, 0, 1, "rk_listed1")
+        copy_rk(0, "q_raw01")
         quantize(0, 0, "q_codes00")
-        cast(nc.scalar.copy, 1, 0, "rk_cols1")
-        cast(nc.vector.tensor_copy, 1, 1, "rk_listed0")
+        part(1, "rk_listed0")
         quantize(0, 1, "q_codes01")
+        cast(nc.scalar.copy, 1, 0, "rk_cols1")
+        cast(nc.vector.tensor_copy, 1, 1, "rk_listed1")
         quantize(1, 1, "q_codes11")
         quantize(1, 0, "q_codes10")
 
@@ -148,17 +155,15 @@ def tile_attend_cosexp_topk_kernel(tc, qT, k_words, k_scales, rk, rq, offs, out)
                 target,
                 lhsT=q_codes[o, c][:].bitcast(FP8X4),
                 lhsT_scale=q_scale[o, c][:],
-                rhs=k_codes[:, o, slots].bitcast(FP4X4),
+                rhs=k_codes[o][:, slots].bitcast(FP4X4),
                 rhs_scale=k_scale[:, o * N + slots.start : o * N + slots.stop],
                 start=start,
                 stop=stop,
             )
 
         for o, c in ((0, 0), (0, 1), (1, 1), (1, 0)):
-            for s in range(N // P):
-                u, j = divmod(s, CHUNK // P)
-                first, last = (o, j) == (0, 0), (o, j) == (PASSES - 1, CHUNK // P - 1)
-                matmul(scores[c, u][:, j * P : (j + 1) * P], o, c, slice(s * P, (s + 1) * P), first, last)
+            for u in range(N // CHUNK):
+                matmul(scores[c, u][:], o, c, slice(u * CHUNK, (u + 1) * CHUNK), o == 0, o == PASSES - 1)
 
         for c in (1, 0):
             for u in range(N // CHUNK):

@@ -22,7 +22,7 @@ P = 128
 PASSES = D // 512
 TILES = NQ // P
 GAIN = 10.0
-SCALE_ROW0 = 96
+SCALE_ROW0 = 32
 HALF = N // 2
 CHUNK = N // 2
 
@@ -44,9 +44,10 @@ def tile_attend_cosexp_topk_kernel(tc, qT, k_words, k_scales, rk, rq, offs, out)
         minus_gain = sb.tile([P, 1], F32, name="minus_gain")
         nc.vector.memset(minus_gain[:], -GAIN)
 
-        scale_pool = sb.tile([P, T + 4], U8, name="scale_pool")
-        nc.sync.dma_start(scale_pool[SCALE_ROW0:P, 0:T].bitcast(I32), k_scales.bitcast(I32).rearrange("o f t -> f o t"))
+        scale_pool = sb.tile([P, T + 4], U8, name="scale_pool", tag="scale_pool", align_bytes=64)
+        nc.sync.dma_start(scale_pool[SCALE_ROW0 : 2 * SCALE_ROW0, 0:T].bitcast(I32), k_scales.bitcast(I32).rearrange("o f t -> f o t"))
         nc.vector.memset(scale_pool[0:SCALE_ROW0, :].bitcast(I32), 0)
+        nc.vector.memset(scale_pool[2 * SCALE_ROW0 : P, :].bitcast(I32), 0)
 
         nc.sync.dma_start(rk_pool[P - 1 : P, :], rk[0:1, :])
 
@@ -58,14 +59,10 @@ def tile_attend_cosexp_topk_kernel(tc, qT, k_words, k_scales, rk, rq, offs, out)
         nc.sync.dma_start(word_pool[:], k_words[0].rearrange("p t b -> p (t b)").bitcast(I32))
 
         q_rows = qT[0].rearrange("(o p t) q -> o p t q", o=PASSES, t=4)
-        q_raw = {}
-        for c in range(TILES):
-            q_raw[0, c] = sb.tile([P, 4, P], F32, name="q_raw0%d" % c, tag="q_raw0%d" % c, align_bytes=64)
-            nc.sync.dma_start(q_raw[0, c][:], q_rows[0][:, :, c * P : (c + 1) * P])
-        q_raw1 = sb.tile([P, 4, NQ], F32, name="q_raw1", tag="q_raw1", align_bytes=64)
-        nc.sync.dma_start(q_raw1[:], q_rows[1])
-        for c in range(TILES):
-            q_raw[1, c] = q_raw1[:, :, c * P : (c + 1) * P]
+        q_raw0 = sb.tile([P, 4, NQ], F32, name="q_raw0", align_bytes=64)
+        nc.sync.dma_start(q_raw0[:], q_rows[0])
+        q_raw1 = [sb.tile([P, 2, NQ], F32, name="q_raw1a", tag="q_raw1a", align_bytes=64)]
+        nc.sync.dma_start(q_raw1[0][:], q_rows[1][:, 0:2, :])
 
         gain = sb.tile([P, 1], F32, name="gain", tag="gain", align_bytes=64)
         nc.scalar.activation(gain[:], minus_gain[:], ACT.Exp, scale=-math.log(GAIN) / GAIN)
@@ -76,9 +73,11 @@ def tile_attend_cosexp_topk_kernel(tc, qT, k_words, k_scales, rk, rq, offs, out)
         nc.vector.tensor_copy(listed_scales[:], scale_pool[:, 0:T].indirect(offsets[:]))
         for u in range(4):
             first = SCALE_ROW0 + 8 * u
-            nc.scalar.dma_start(
+            nc.sync.dma_start(
                 k_scale[32 * u : 32 * u + 4, 0 : PASSES * N].bitcast(I32), listed_scales[first : first + 8, :].bitcast(I32)
             )
+        q_raw1.append(sb.tile([P, 2, NQ], F32, name="q_raw1b", tag="scale_pool", align_bytes=64))
+        nc.sync.dma_start(q_raw1[1][:], q_rows[1][:, 2:4, :])
 
         rq_turned = ps.tile([P, P], F32, name="rq_turned", tag="bank1")
         nc.tensor.transpose(rq_turned[:], rq_rows[:, 0:P], ident[:])
@@ -89,7 +88,7 @@ def tile_attend_cosexp_topk_kernel(tc, qT, k_words, k_scales, rk, rq, offs, out)
         rk_cols = []
         for h in range(2):
             rk_listed = sb.tile([P, HALF], F32, name="rk_listed%d" % h, tag="rk_listed%d" % h, align_bytes=64)
-            nc.vector.tensor_copy(rk_listed[:], rk_pool[:].indirect(offsets[:, h * HALF // 16 : (h + 1) * HALF // 16]))
+            nc.scalar.activation(rk_listed[:], rk_pool[:].indirect(offsets[:, h * HALF // 16 : (h + 1) * HALF // 16]), ACT.Copy)
             rk_turned = ps.tile([P, HALF // P, P], F32, name="rk_turned%d" % h, tag="bank%d" % (2 * h))
             for s in range(HALF // P):
                 nc.tensor.transpose(rk_turned[:, s, :], rk_listed[:, s * P : (s + 1) * P], ident[:])
@@ -123,10 +122,11 @@ def tile_attend_cosexp_topk_kernel(tc, qT, k_words, k_scales, rk, rq, offs, out)
 
         def cast(copy, o, c, tag):
             q_bf[o, c] = sb.tile([P, P, 4], BF16, name="q_bf%d%d" % (o, c), tag=tag, align_bytes=64)
-            copy(
-                q_bf[o, c][:].rearrange("p (g i) t -> p g t i", i=4),
-                q_raw[o, c][:].rearrange("p t (g i) -> p g t i", i=4),
-            )
+            for raw, rows in ((q_raw0, slice(0, 4)),) if o == 0 else ((q_raw1[0], slice(0, 2)), (q_raw1[1], slice(2, 4))):
+                copy(
+                    q_bf[o, c][:].rearrange("p (g i) t -> p g t i", i=4)[:, :, rows, :],
+                    raw[:, :, c * P : (c + 1) * P].rearrange("p t (g i) -> p g t i", i=4),
+                )
 
         def quantize(o, c, tag):
             q_codes[o, c] = sb.tile([P, P], U32, name="q_codes%d%d" % (o, c), tag=tag, align_bytes=64)
@@ -135,16 +135,16 @@ def tile_attend_cosexp_topk_kernel(tc, qT, k_words, k_scales, rk, rq, offs, out)
 
         cast(nc.scalar.copy, 0, 0, "rk_listed0")
         cast(nc.scalar.copy, 0, 1, "rk_listed1")
-        copy_rk(0, "q_raw01")
+        copy_rk(0, "gain")
         quantize(0, 0, "q_codes00")
-        part(1, "rk_listed0")
-        quantize(0, 1, "q_codes01")
+        part(1, "k_codes1")
         cast(nc.scalar.copy, 1, 0, "rk_cols1")
-        cast(nc.vector.tensor_copy, 1, 1, "rk_listed1")
+        cast(nc.vector.tensor_copy, 1, 1, "rk_listed0")
+        quantize(0, 1, "q_codes01")
         quantize(1, 1, "q_codes11")
         quantize(1, 0, "q_codes10")
 
-        copy_rk(1, "q_raw1")
+        copy_rk(1, "q_raw1a")
 
         scores = {}
         for c, u, tag in ((0, 0, "bank2"), (0, 1, "bank3"), (1, 0, "bank0"), (1, 1, "bank1")):

@@ -33,50 +33,50 @@ def tile_attend_cosexp_topk_kernel(tc, qT, k_words, k_scales, rk, rq, offs, out)
         sb = ctx.enter_context(tc.tile_pool(name="sb", bufs=1))
         ps = ctx.enter_context(tc.psum_pool(name="ps", bufs=1))
 
-        offsets = sb.tile([P, N // 16], U16, name="offsets")
+        offsets = sb.tile([P, N // 16], U16, name="offsets", align_bytes=256)
         nc.sync.dma_start(offsets[:], offs)
 
-        rk_pool = sb.tile([P, T], F32, name="rk_pool")
+        rk_pool = sb.tile([P, T], F32, name="rk_pool", align_bytes=256)
         nc.gpsimd.memset(rk_pool[0 : P - 1, :], 0.0)
 
-        ident = sb.tile([P, P], F32, name="ident", tag="ident", align_bytes=64)
+        ident = sb.tile([P, P], F32, name="ident", tag="ident", align_bytes=256)
         make_identity(nc, ident[:])
         minus_gain = sb.tile([P, 1], F32, name="minus_gain")
         nc.vector.memset(minus_gain[:], -GAIN)
 
-        scale_pool = sb.tile([P, T + 4], U8, name="scale_pool", tag="scale_pool", align_bytes=64)
+        scale_pool = sb.tile([P, T + 4], U8, name="scale_pool", tag="scale_pool", align_bytes=256)
         nc.sync.dma_start(scale_pool[SCALE_ROW0 : 2 * SCALE_ROW0, 0:T].bitcast(I32), k_scales.bitcast(I32).rearrange("o f t -> f o t"))
         nc.vector.memset(scale_pool[0:SCALE_ROW0, :].bitcast(I32), 0)
         nc.vector.memset(scale_pool[2 * SCALE_ROW0 : P, :].bitcast(I32), 0)
 
         nc.sync.dma_start(rk_pool[P - 1 : P, :], rk[0:1, :])
 
-        rq_rows = sb.tile([P, P + 1], F32, name="rq_rows")
+        rq_rows = sb.tile([P, P + 1], F32, name="rq_rows", align_bytes=256)
         nc.vector.memset(rq_rows[0 : P - TILES, :], 0.0)
         nc.scalar.dma_start(rq_rows[P - TILES : P, 0:P], rq[0].rearrange("(c q) one -> c (q one)", c=TILES))
 
-        word_pool = sb.tile([P, T], I32, name="word_pool", tag="word_pool", align_bytes=64)
+        word_pool = sb.tile([P, T], I32, name="word_pool", tag="word_pool", align_bytes=256)
         nc.sync.dma_start(word_pool[:], k_words[0].rearrange("p t b -> p (t b)").bitcast(I32))
 
         q_rows = qT[0].rearrange("(o p t) q -> o p t q", o=PASSES, t=4)
-        q_raw0 = sb.tile([P, 4, NQ], F32, name="q_raw0", align_bytes=64)
+        q_raw0 = sb.tile([P, 4, NQ], F32, name="q_raw0", align_bytes=256)
         nc.sync.dma_start(q_raw0[:], q_rows[0])
-        q_raw1 = [sb.tile([P, 2, NQ], F32, name="q_raw1a", tag="q_raw1a", align_bytes=64)]
+        q_raw1 = [sb.tile([P, 2, NQ], F32, name="q_raw1a", tag="q_raw1a", align_bytes=256)]
         nc.sync.dma_start(q_raw1[0][:], q_rows[1][:, 0:2, :])
 
-        gain = sb.tile([P, 1], F32, name="gain", tag="gain", align_bytes=64)
+        gain = sb.tile([P, 1], F32, name="gain", tag="gain", align_bytes=256)
         nc.scalar.activation(gain[:], minus_gain[:], ACT.Exp, scale=-math.log(GAIN) / GAIN)
 
-        k_scale = sb.tile([P, PASSES * N + 4], U8, name="k_scale", align_bytes=64)
+        k_scale = sb.tile([P, PASSES * N + 4], U8, name="k_scale", align_bytes=256)
         nc.vector.memset(k_scale[:].bitcast(I32), 0)
-        listed_scales = sb.tile([P, N], U8, name="listed_scales")
+        listed_scales = sb.tile([P, N], U8, name="listed_scales", align_bytes=256)
         nc.vector.tensor_copy(listed_scales[:], scale_pool[:, 0:T].indirect(offsets[:]))
         for u in range(4):
             first = SCALE_ROW0 + 8 * u
             nc.sync.dma_start(
                 k_scale[32 * u : 32 * u + 4, 0 : PASSES * N].bitcast(I32), listed_scales[first : first + 8, :].bitcast(I32)
             )
-        q_raw1.append(sb.tile([P, 2, NQ], F32, name="q_raw1b", tag="scale_pool", align_bytes=64))
+        q_raw1.append(sb.tile([P, 2, NQ], F32, name="q_raw1b", tag="scale_pool", align_bytes=256))
         nc.sync.dma_start(q_raw1[1][:], q_rows[1][:, 2:4, :])
 
         rq_turned = ps.tile([P, P], F32, name="rq_turned", tag="bank1")
@@ -87,18 +87,18 @@ def tile_attend_cosexp_topk_kernel(tc, qT, k_words, k_scales, rk, rq, offs, out)
         rk_spread = [ps.tile([P, HALF], F32, name="rk_spread%d" % h) for h in range(2)]
         rk_cols = []
         for h in range(2):
-            rk_listed = sb.tile([P, HALF], F32, name="rk_listed%d" % h, tag="rk_listed%d" % h, align_bytes=64)
+            rk_listed = sb.tile([P, HALF], F32, name="rk_listed%d" % h, tag="rk_listed%d" % h, align_bytes=256)
             nc.scalar.activation(rk_listed[:], rk_pool[:].indirect(offsets[:, h * HALF // 16 : (h + 1) * HALF // 16]), ACT.Copy)
             rk_turned = ps.tile([P, HALF // P, P], F32, name="rk_turned%d" % h, tag="bank%d" % (2 * h))
             for s in range(HALF // P):
                 nc.tensor.transpose(rk_turned[:, s, :], rk_listed[:, s * P : (s + 1) * P], ident[:])
-            rk_cols.append(sb.tile([P, HALF // P], F32, name="rk_cols%d" % h, tag="rk_cols%d" % h, align_bytes=64))
+            rk_cols.append(sb.tile([P, HALF // P], F32, name="rk_cols%d" % h, tag="rk_cols%d" % h, align_bytes=256))
             nc.scalar.activation(rk_cols[h][:], rk_turned[:, :, P - 1], ACT.Copy, scale=gain[:])
         for s in range(N // P):
             column = rk_cols[s * P // HALF][:, s % (HALF // P) : s % (HALF // P) + 1]
             nc.tensor.transpose(rk_spread[s * P // HALF][:, s * P % HALF : s * P % HALF + P], column.to_broadcast([P, P]), ident[:])
 
-        listed_words = sb.tile([P, N], U32, name="listed_words", tag="listed_words", align_bytes=64)
+        listed_words = sb.tile([P, N], U32, name="listed_words", tag="listed_words", align_bytes=256)
         for h in range(2):
             nc.vector.tensor_copy(
                 listed_words[:, h * HALF : (h + 1) * HALF],
@@ -107,7 +107,7 @@ def tile_attend_cosexp_topk_kernel(tc, qT, k_words, k_scales, rk, rq, offs, out)
         k_codes = {}
 
         def part(o, tag):
-            k_codes[o] = sb.tile([P, N], U16, name="k_codes%d" % o, tag=tag, align_bytes=64)
+            k_codes[o] = sb.tile([P, N], U16, name="k_codes%d" % o, tag=tag, align_bytes=256)
             nc.vector.tensor_copy(k_codes[o][:], listed_words[:].bitcast(U16).rearrange("p (n o) -> p o n", o=PASSES)[:, o, :])
 
         part(0, "k_codes0")
@@ -115,13 +115,13 @@ def tile_attend_cosexp_topk_kernel(tc, qT, k_words, k_scales, rk, rq, offs, out)
         rk_rows = {}
 
         def copy_rk(h, tag):
-            rk_rows[h] = sb.tile([P, HALF], F32, name="rk_rows%d" % h, tag=tag, align_bytes=64)
+            rk_rows[h] = sb.tile([P, HALF], F32, name="rk_rows%d" % h, tag=tag, align_bytes=256)
             nc.scalar.copy(rk_rows[h][:], rk_spread[h][:])
 
         q_bf, q_codes, q_scale = {}, {}, {}
 
         def cast(copy, o, c, tag):
-            q_bf[o, c] = sb.tile([P, P, 4], BF16, name="q_bf%d%d" % (o, c), tag=tag, align_bytes=64)
+            q_bf[o, c] = sb.tile([P, P, 4], BF16, name="q_bf%d%d" % (o, c), tag=tag, align_bytes=256)
             for raw, rows in ((q_raw0, slice(0, 4)),) if o == 0 else ((q_raw1[0], slice(0, 2)), (q_raw1[1], slice(2, 4))):
                 copy(
                     q_bf[o, c][:].rearrange("p (g i) t -> p g t i", i=4)[:, :, rows, :],
@@ -129,8 +129,8 @@ def tile_attend_cosexp_topk_kernel(tc, qT, k_words, k_scales, rk, rq, offs, out)
                 )
 
         def quantize(o, c, tag):
-            q_codes[o, c] = sb.tile([P, P], U32, name="q_codes%d%d" % (o, c), tag=tag, align_bytes=64)
-            q_scale[o, c] = sb.tile([P, P], U8, name="q_scale%d%d" % (o, c), align_bytes=64)
+            q_codes[o, c] = sb.tile([P, P], U32, name="q_codes%d%d" % (o, c), tag=tag, align_bytes=256)
+            q_scale[o, c] = sb.tile([P, P], U8, name="q_scale%d%d" % (o, c), align_bytes=256)
             nc.vector.quantize_mx(q_codes[o, c][:].bitcast(FP8X4), q_scale[o, c][:], q_bf[o, c][:].rearrange("p q t -> p (q t)"))
 
         cast(nc.scalar.copy, 0, 0, "rk_listed0")
@@ -168,8 +168,8 @@ def tile_attend_cosexp_topk_kernel(tc, qT, k_words, k_scales, rk, rq, offs, out)
         for c in (1, 0):
             for u in range(N // CHUNK):
                 slots = slice(u * CHUNK, (u + 1) * CHUNK)
-                scaled = sb.tile([P, CHUNK], F32, name="scaled%d%d" % (c, u))
+                scaled = sb.tile([P, CHUNK], F32, name="scaled%d%d" % (c, u), align_bytes=256)
                 nc.vector.tensor_tensor(scaled[:], scores[c, u][:], rk_rows[u][:], MULT)
-                result = sb.tile([P, CHUNK], F32, name="result%d%d" % (c, u))
+                result = sb.tile([P, CHUNK], F32, name="result%d%d" % (c, u), align_bytes=256)
                 nc.scalar.activation(result[:], scaled[:], ACT.Exp, bias=minus_gain[:], scale=rq_cols[:, c : c + 1])
                 nc.sync.dma_start(out[0, c * P : (c + 1) * P, slots], result[:])

@@ -31,16 +31,16 @@ def tile_attend_cosexp_topk_kernel(tc, qT, k_words, k_scales, rk, rq, offs, out)
     nc = tc.nc
     with ExitStack() as ctx:
         sb = ctx.enter_context(tc.tile_pool(name="sb", bufs=1))
+        turns = ctx.enter_context(tc.tile_pool(name="turns", bufs=1))
         ps = ctx.enter_context(tc.psum_pool(name="ps", bufs=1))
 
         offsets = sb.tile([P, N // 16], U16, name="offsets", align_bytes=256)
         nc.sync.dma_start(offsets[:], offs)
 
-        rk_pool = sb.tile([P, T], F32, name="rk_pool", align_bytes=256)
-        nc.gpsimd.memset(rk_pool[0 : P - 1, :], 0.0)
-
         ident = sb.tile([P, P], F32, name="ident", tag="ident", align_bytes=256)
         make_identity(nc, ident[:])
+        rk_pool = sb.tile([P, T], F32, name="rk_pool", tag="rk_pool", align_bytes=256)
+        nc.gpsimd.memset(rk_pool[0 : P - 1, :], 0.0)
         minus_gain = sb.tile([P, 1], F32, name="minus_gain")
         nc.vector.memset(minus_gain[:], -GAIN)
 
@@ -87,30 +87,33 @@ def tile_attend_cosexp_topk_kernel(tc, qT, k_words, k_scales, rk, rq, offs, out)
         rk_spread = [ps.tile([P, HALF], F32, name="rk_spread%d" % h) for h in range(2)]
         rk_cols = []
         for h in range(2):
-            rk_listed = sb.tile([P, HALF], F32, name="rk_listed%d" % h, tag="rk_listed%d" % h, align_bytes=256)
-            nc.scalar.activation(rk_listed[:], rk_pool[:].indirect(offsets[:, h * HALF // 16 : (h + 1) * HALF // 16]), ACT.Copy)
+            rk_listed = turns.tile([P, HALF], F32, name="rk_listed%d" % h, align_bytes=256, offset=(2048, 512)[h])
+            listed = rk_pool[:].indirect(offsets[:, h * HALF // 16 : (h + 1) * HALF // 16])
+            if h == 0:
+                nc.scalar.activation(rk_listed[:], listed, ACT.Copy)
+            else:
+                nc.vector.tensor_copy(rk_listed[:], listed)
             rk_turned = ps.tile([P, HALF // P, P], F32, name="rk_turned%d" % h, tag="bank%d" % (2 * h))
             for s in range(HALF // P):
                 nc.tensor.transpose(rk_turned[:, s, :], rk_listed[:, s * P : (s + 1) * P], ident[:])
-            rk_cols.append(sb.tile([P, HALF // P], F32, name="rk_cols%d" % h, tag="rk_cols%d" % h, align_bytes=256))
+            rk_cols.append(turns.tile([P, HALF // P], F32, name="rk_cols%d" % h, align_bytes=256, offset=(4096, 3072)[h]))
             nc.scalar.activation(rk_cols[h][:], rk_turned[:, :, P - 1], ACT.Copy, scale=gain[:])
         for s in range(N // P):
             column = rk_cols[s * P // HALF][:, s % (HALF // P) : s % (HALF // P) + 1]
             nc.tensor.transpose(rk_spread[s * P // HALF][:, s * P % HALF : s * P % HALF + P], column.to_broadcast([P, P]), ident[:])
 
-        listed_words = sb.tile([P, N], U32, name="listed_words", tag="listed_words", align_bytes=256)
+        listed_words = sb.tile([P, N], U32, name="listed_words", tag="rk_pool", align_bytes=256)
         for h in range(2):
             nc.vector.tensor_copy(
                 listed_words[:, h * HALF : (h + 1) * HALF],
                 word_pool[:].bitcast(U32).indirect(offsets[:, h * HALF // 16 : (h + 1) * HALF // 16]),
             )
-        k_codes = {}
-
-        def part(o, tag):
-            k_codes[o] = sb.tile([P, N], U16, name="k_codes%d" % o, tag=tag, align_bytes=256)
-            nc.vector.tensor_copy(k_codes[o][:], listed_words[:].bitcast(U16).rearrange("p (n o) -> p o n", o=PASSES)[:, o, :])
-
-        part(0, "k_codes0")
+        k_codes = sb.tile([P, PASSES, N], U16, name="k_codes", align_bytes=256)
+        for h in range(2):
+            nc.vector.tensor_copy(
+                k_codes[:, :, h * HALF : (h + 1) * HALF],
+                listed_words[:, h * HALF : (h + 1) * HALF].bitcast(U16).rearrange("p (n o) -> p o n", o=PASSES),
+            )
 
         rk_rows = {}
 
@@ -120,8 +123,8 @@ def tile_attend_cosexp_topk_kernel(tc, qT, k_words, k_scales, rk, rq, offs, out)
 
         q_bf, q_codes, q_scale = {}, {}, {}
 
-        def cast(copy, o, c, tag):
-            q_bf[o, c] = sb.tile([P, P, 4], BF16, name="q_bf%d%d" % (o, c), tag=tag, align_bytes=256)
+        def cast(copy, o, c, offset):
+            q_bf[o, c] = turns.tile([P, P, 4], BF16, name="q_bf%d%d" % (o, c), align_bytes=256, offset=offset)
             for raw, rows in ((q_raw0, slice(0, 4)),) if o == 0 else ((q_raw1[0], slice(0, 2)), (q_raw1[1], slice(2, 4))):
                 copy(
                     q_bf[o, c][:].rearrange("p (g i) t -> p g t i", i=4)[:, :, rows, :],
@@ -133,13 +136,12 @@ def tile_attend_cosexp_topk_kernel(tc, qT, k_words, k_scales, rk, rq, offs, out)
             q_scale[o, c] = sb.tile([P, P], U8, name="q_scale%d%d" % (o, c), align_bytes=256)
             nc.vector.quantize_mx(q_codes[o, c][:].bitcast(FP8X4), q_scale[o, c][:], q_bf[o, c][:].rearrange("p q t -> p (q t)"))
 
-        cast(nc.scalar.copy, 0, 0, "rk_listed0")
-        cast(nc.scalar.copy, 0, 1, "rk_listed1")
+        cast(nc.scalar.copy, 0, 0, 0)
+        cast(nc.scalar.copy, 0, 1, 1024)
         copy_rk(0, "gain")
         quantize(0, 0, "q_codes00")
-        part(1, "k_codes1")
-        cast(nc.scalar.copy, 1, 0, "rk_cols1")
-        cast(nc.vector.tensor_copy, 1, 1, "rk_listed0")
+        cast(nc.scalar.copy, 1, 0, 3072)
+        cast(nc.vector.tensor_copy, 1, 1, 0)
         quantize(0, 1, "q_codes01")
         quantize(1, 1, "q_codes11")
         quantize(1, 0, "q_codes10")
@@ -155,7 +157,7 @@ def tile_attend_cosexp_topk_kernel(tc, qT, k_words, k_scales, rk, rq, offs, out)
                 target,
                 lhsT=q_codes[o, c][:].bitcast(FP8X4),
                 lhsT_scale=q_scale[o, c][:],
-                rhs=k_codes[o][:, slots].bitcast(FP4X4),
+                rhs=k_codes[:, o, slots].bitcast(FP4X4),
                 rhs_scale=k_scale[:, o * N + slots.start : o * N + slots.stop],
                 start=start,
                 stop=stop,

@@ -39,7 +39,7 @@ def tile_attend_cosexp_topk_kernel(tc, qT, k_words, k_scales, rk, rq, offs, out)
 
         ident = sb.tile([P, P], F32, name="ident", tag="ident", align_bytes=256)
         make_identity(nc, ident[:])
-        rk_pool = sb.tile([P, T], F32, name="rk_pool", tag="rk_pool", align_bytes=256)
+        rk_pool = turns.tile([P, T], F32, name="rk_pool", align_bytes=256, offset=20480)
         nc.gpsimd.memset(rk_pool[0 : P - 1, :], 0.0)
         minus_gain = sb.tile([P, 1], F32, name="minus_gain")
         nc.vector.memset(minus_gain[:], -GAIN)
@@ -59,25 +59,16 @@ def tile_attend_cosexp_topk_kernel(tc, qT, k_words, k_scales, rk, rq, offs, out)
         nc.sync.dma_start(word_pool[:], k_words[0].rearrange("p t b -> p (t b)").bitcast(I32))
 
         q_rows = qT[0].rearrange("(o p t) q -> o p t q", o=PASSES, t=4)
-        q_raw0 = sb.tile([P, 4, NQ], F32, name="q_raw0", align_bytes=256)
-        nc.sync.dma_start(q_raw0[:], q_rows[0])
-        q_raw1 = [sb.tile([P, 2, NQ], F32, name="q_raw1a", tag="q_raw1a", align_bytes=256)]
-        nc.sync.dma_start(q_raw1[0][:], q_rows[1][:, 0:2, :])
+        q_raw = []
+        for o in range(PASSES):
+            q_raw.append(turns.tile([P, 4, NQ], F32, name="q_raw%d" % o, align_bytes=256, offset=12288 + 4096 * o))
+            nc.sync.dma_start(q_raw[o][:], q_rows[o])
 
         gain = sb.tile([P, 1], F32, name="gain", tag="gain", align_bytes=256)
         nc.scalar.activation(gain[:], minus_gain[:], ACT.Exp, scale=-math.log(GAIN) / GAIN)
 
-        k_scale = sb.tile([P, PASSES * N + 4], U8, name="k_scale", align_bytes=256)
-        nc.vector.memset(k_scale[:].bitcast(I32), 0)
         listed_scales = sb.tile([P, N], U8, name="listed_scales", align_bytes=256)
         nc.vector.tensor_copy(listed_scales[:], scale_pool[:, 0:T].indirect(offsets[:]))
-        for u in range(4):
-            first = SCALE_ROW0 + 8 * u
-            nc.sync.dma_start(
-                k_scale[32 * u : 32 * u + 4, 0 : PASSES * N].bitcast(I32), listed_scales[first : first + 8, :].bitcast(I32)
-            )
-        q_raw1.append(sb.tile([P, 2, NQ], F32, name="q_raw1b", tag="scale_pool", align_bytes=256))
-        nc.sync.dma_start(q_raw1[1][:], q_rows[1][:, 2:4, :])
 
         rq_turned = ps.tile([P, P], F32, name="rq_turned", tag="bank1")
         nc.tensor.transpose(rq_turned[:], rq_rows[:, 0:P], ident[:])
@@ -102,7 +93,14 @@ def tile_attend_cosexp_topk_kernel(tc, qT, k_words, k_scales, rk, rq, offs, out)
             column = rk_cols[s * P // HALF][:, s % (HALF // P) : s % (HALF // P) + 1]
             nc.tensor.transpose(rk_spread[s * P // HALF][:, s * P % HALF : s * P % HALF + P], column.to_broadcast([P, P]), ident[:])
 
-        listed_words = sb.tile([P, N], U32, name="listed_words", tag="rk_pool", align_bytes=256)
+        k_scale = turns.tile([P, PASSES * N], U8, name="k_scale", align_bytes=256, offset=24576)
+        for u in range(4):
+            first = SCALE_ROW0 + 8 * u
+            nc.scalar.dma_start(
+                k_scale[32 * u : 32 * u + 4, 0 : PASSES * N].bitcast(I32), listed_scales[first : first + 8, :].bitcast(I32)
+            )
+
+        listed_words = turns.tile([P, N], U32, name="listed_words", align_bytes=256, offset=20480)
         for h in range(2):
             nc.vector.tensor_copy(
                 listed_words[:, h * HALF : (h + 1) * HALF],
@@ -117,36 +115,35 @@ def tile_attend_cosexp_topk_kernel(tc, qT, k_words, k_scales, rk, rq, offs, out)
 
         rk_rows = {}
 
-        def copy_rk(h, tag):
-            rk_rows[h] = sb.tile([P, HALF], F32, name="rk_rows%d" % h, tag=tag, align_bytes=256)
+        def copy_rk(h, offset):
+            rk_rows[h] = turns.tile([P, HALF], F32, name="rk_rows%d" % h, align_bytes=256, offset=offset)
             nc.scalar.copy(rk_rows[h][:], rk_spread[h][:])
 
         q_bf, q_codes, q_scale = {}, {}, {}
 
-        def cast(copy, o, c, offset):
-            q_bf[o, c] = turns.tile([P, P, 4], BF16, name="q_bf%d%d" % (o, c), align_bytes=256, offset=offset)
-            for raw, rows in ((q_raw0, slice(0, 4)),) if o == 0 else ((q_raw1[0], slice(0, 2)), (q_raw1[1], slice(2, 4))):
-                copy(
-                    q_bf[o, c][:].rearrange("p (g i) t -> p g t i", i=4)[:, :, rows, :],
-                    raw[:, :, c * P : (c + 1) * P].rearrange("p t (g i) -> p g t i", i=4),
-                )
+        def cast(copy, o, c, queries):
+            copy(
+                q_bf[o, c][:, queries, :].rearrange("p (g i) t -> p g t i", i=4),
+                q_raw[o][:, :, c * P + queries.start : c * P + queries.stop].rearrange("p t (g i) -> p g t i", i=4),
+            )
 
-        def quantize(o, c, tag):
-            q_codes[o, c] = sb.tile([P, P], U32, name="q_codes%d%d" % (o, c), tag=tag, align_bytes=256)
+        def quantize(o, c, offset):
+            q_codes[o, c] = turns.tile([P, P], U32, name="q_codes%d%d" % (o, c), align_bytes=256, offset=offset)
             q_scale[o, c] = sb.tile([P, P], U8, name="q_scale%d%d" % (o, c), align_bytes=256)
             nc.vector.quantize_mx(q_codes[o, c][:].bitcast(FP8X4), q_scale[o, c][:], q_bf[o, c][:].rearrange("p q t -> p (q t)"))
 
-        cast(nc.scalar.copy, 0, 0, 0)
-        cast(nc.scalar.copy, 0, 1, 1024)
-        copy_rk(0, "gain")
-        quantize(0, 0, "q_codes00")
-        cast(nc.scalar.copy, 1, 0, 3072)
-        cast(nc.vector.tensor_copy, 1, 1, 0)
-        quantize(0, 1, "q_codes01")
-        quantize(1, 1, "q_codes11")
-        quantize(1, 0, "q_codes10")
-
-        copy_rk(1, "q_raw1a")
+        for o, c, offset in ((0, 0, 0), (0, 1, 1024), (1, 0, 3072), (1, 1, 0)):
+            q_bf[o, c] = turns.tile([P, P, 4], BF16, name="q_bf%d%d" % (o, c), align_bytes=256, offset=offset)
+        cast(nc.scalar.copy, 0, 0, slice(0, P))
+        cast(nc.scalar.copy, 0, 1, slice(0, P))
+        copy_rk(0, 12288)
+        quantize(0, 0, 8192)
+        cast(nc.scalar.copy, 1, 0, slice(0, P))
+        cast(nc.vector.tensor_copy, 1, 1, slice(0, P))
+        quantize(0, 1, 8704)
+        quantize(1, 1, 9216)
+        quantize(1, 0, 9728)
+        copy_rk(1, 16384)
 
         scores = {}
         for c, u, tag in ((0, 0, "bank2"), (0, 1, "bank3"), (1, 0, "bank0"), (1, 1, "bank1")):

@@ -62,7 +62,8 @@ def tile_attend_cosexp_topk_kernel(tc, qT, k_words, k_scales, rk, rq, offs, out)
         q_raw = []
         for o in range(PASSES):
             q_raw.append(turns.tile([P, 4, NQ], F32, name="q_raw%d" % o, align_bytes=256, offset=12288 + 4096 * o))
-            nc.sync.dma_start(q_raw[o][:], q_rows[o])
+        nc.sync.dma_start(q_raw[0][:], q_rows[0])
+        nc.sync.dma_start(q_raw[1][:, 0:2, :], q_rows[1][:, 0:2, :])
 
         gain = sb.tile([P, 1], F32, name="gain", tag="gain", align_bytes=256)
         nc.scalar.activation(gain[:], minus_gain[:], ACT.Exp, scale=-math.log(GAIN) / GAIN)
@@ -78,12 +79,12 @@ def tile_attend_cosexp_topk_kernel(tc, qT, k_words, k_scales, rk, rq, offs, out)
         rk_spread = [ps.tile([P, HALF], F32, name="rk_spread%d" % h) for h in range(2)]
         rk_cols = []
         for h in range(2):
-            rk_listed = turns.tile([P, HALF], F32, name="rk_listed%d" % h, align_bytes=256, offset=(2048, 512)[h])
+            rk_listed = q_raw[1][:, 3, :] if h == 0 else turns.tile([P, HALF], F32, name="rk_listed1", align_bytes=256, offset=512)[:]
             listed = rk_pool[:].indirect(offsets[:, h * HALF // 16 : (h + 1) * HALF // 16])
             if h == 0:
-                nc.scalar.activation(rk_listed[:], listed, ACT.Copy)
+                nc.scalar.activation(rk_listed, listed, ACT.Copy)
             else:
-                nc.vector.tensor_copy(rk_listed[:], listed)
+                nc.vector.tensor_copy(rk_listed, listed)
             rk_turned = ps.tile([P, HALF // P, P], F32, name="rk_turned%d" % h, tag="bank%d" % (2 * h))
             for s in range(HALF // P):
                 nc.tensor.transpose(rk_turned[:, s, :], rk_listed[:, s * P : (s + 1) * P], ident[:])
@@ -93,12 +94,14 @@ def tile_attend_cosexp_topk_kernel(tc, qT, k_words, k_scales, rk, rq, offs, out)
             column = rk_cols[s * P // HALF][:, s % (HALF // P) : s % (HALF // P) + 1]
             nc.tensor.transpose(rk_spread[s * P // HALF][:, s * P % HALF : s * P % HALF + P], column.to_broadcast([P, P]), ident[:])
 
-        k_scale = turns.tile([P, PASSES * N], U8, name="k_scale", align_bytes=256, offset=24576)
+        k_scale = sb.tile([P, PASSES * N], U8, name="k_scale", align_bytes=256)
         for u in range(4):
             first = SCALE_ROW0 + 8 * u
-            nc.scalar.dma_start(
+            nc.sync.dma_start(
                 k_scale[32 * u : 32 * u + 4, 0 : PASSES * N].bitcast(I32), listed_scales[first : first + 8, :].bitcast(I32)
             )
+
+        nc.sync.dma_start(q_raw[1][:, 2:4, :], q_rows[1][:, 2:4, :])
 
         listed_words = turns.tile([P, N], U32, name="listed_words", align_bytes=256, offset=20480)
         for h in range(2):

@@ -25,6 +25,7 @@ GAIN = 10.0
 SCALE_ROW0 = 32
 HALF = N // 2
 CHUNK = N // 2
+STEP = 128
 
 
 def tile_attend_cosexp_topk_kernel(tc, qT, k_words, k_scales, rk, rq, offs, out):
@@ -135,43 +136,46 @@ def tile_attend_cosexp_topk_kernel(tc, qT, k_words, k_scales, rk, rq, offs, out)
             q_scale[o, c] = sb.tile([P, P], U8, name="q_scale%d%d" % (o, c), align_bytes=256)
             nc.vector.quantize_mx(q_codes[o, c][:].bitcast(FP8X4), q_scale[o, c][:], q_bf[o, c][:].rearrange("p q t -> p (q t)"))
 
-        for o, c, offset in ((0, 0, 0), (0, 1, 1024), (1, 0, 3072), (1, 1, 0)):
+        for o, c, offset in ((0, 0, 0), (0, 1, 1024), (1, 0, 13312), (1, 1, 3072)):
             q_bf[o, c] = turns.tile([P, P, 4], BF16, name="q_bf%d%d" % (o, c), align_bytes=256, offset=offset)
         cast(nc.scalar.copy, 0, 0, slice(0, P))
         cast(nc.scalar.copy, 0, 1, slice(0, P))
         copy_rk(0, 12288)
         quantize(0, 0, 8192)
-        cast(nc.scalar.copy, 1, 0, slice(0, P))
-        cast(nc.vector.tensor_copy, 1, 1, slice(0, P))
         quantize(0, 1, 8704)
-        quantize(1, 1, 9216)
-        quantize(1, 0, 9728)
+        cast(nc.vector.tensor_copy, 1, 0, slice(0, P))
+        cast(nc.scalar.copy, 1, 1, slice(0, P))
+        quantize(1, 0, 9216)
+        quantize(1, 1, 9728)
         copy_rk(1, 16384)
 
+        pieces = ((0, 0, STEP, "bank2"), (0, STEP, STEP, "bank4"), (0, CHUNK, CHUNK, "bank3"), (1, 0, CHUNK, "bank0"), (1, CHUNK, CHUNK, "bank1"))
         scores = {}
-        for c, u, tag in ((0, 0, "bank2"), (0, 1, "bank3"), (1, 0, "bank0"), (1, 1, "bank1")):
-            scores[c, u] = ps.tile([P, CHUNK], F32, name="scores%d%d" % (c, u), tag=tag)
+        for c, first, width, tag in pieces:
+            bank = ps.tile([P, width], F32, name="scores%d_%d" % (c, first), tag=tag)
+            for s in range(0, width, STEP):
+                scores[c, first + s] = bank[:, s : s + STEP]
+            scores[c, first, width] = bank[:]
 
-        def matmul(target, o, c, slots, start, stop):
-            nc.tensor.matmul_mx(
-                target,
-                lhsT=q_codes[o, c][:].bitcast(FP8X4),
-                lhsT_scale=q_scale[o, c][:],
-                rhs=k_codes[:, o, slots].bitcast(FP4X4),
-                rhs_scale=k_scale[:, o * N + slots.start : o * N + slots.stop],
-                start=start,
-                stop=stop,
-            )
+        for o in range(PASSES):
+            for c, first, width, tag in pieces:
+                nc.tensor.matmul_mx(
+                    scores[c, first, width],
+                    lhsT=q_codes[o, c][:].bitcast(FP8X4),
+                    lhsT_scale=q_scale[o, c][:],
+                    rhs=k_codes[:, o, first : first + width].bitcast(FP4X4),
+                    rhs_scale=k_scale[:, o * N + first : o * N + first + width],
+                    start=o == 0,
+                    stop=o == PASSES - 1,
+                )
 
-        for o, c in ((0, 0), (0, 1), (1, 1), (1, 0)):
+        for c in range(TILES):
             for u in range(N // CHUNK):
-                matmul(scores[c, u][:], o, c, slice(u * CHUNK, (u + 1) * CHUNK), o == 0, o == PASSES - 1)
-
-        for c in (1, 0):
-            for u in range(N // CHUNK):
-                slots = slice(u * CHUNK, (u + 1) * CHUNK)
                 scaled = sb.tile([P, CHUNK], F32, name="scaled%d%d" % (c, u), align_bytes=256)
-                nc.vector.tensor_tensor(scaled[:], scores[c, u][:], rk_rows[u][:], MULT)
                 result = sb.tile([P, CHUNK], F32, name="result%d%d" % (c, u), align_bytes=256)
-                nc.scalar.activation(result[:], scaled[:], ACT.Exp, bias=minus_gain[:], scale=rq_cols[:, c : c + 1])
-                nc.sync.dma_start(out[0, c * P : (c + 1) * P, slots], result[:])
+                for s in range(0, CHUNK, STEP):
+                    nc.vector.tensor_tensor(scaled[:, s : s + STEP], scores[c, u * CHUNK + s], rk_rows[u][:, s : s + STEP], MULT)
+                    nc.scalar.activation(
+                        result[:, s : s + STEP], scaled[:, s : s + STEP], ACT.Exp, bias=minus_gain[:], scale=rq_cols[:, c : c + 1]
+                    )
+                nc.sync.dma_start(out[0, c * P : (c + 1) * P, u * CHUNK : (u + 1) * CHUNK], result[:])

@@ -25,6 +25,7 @@ GAIN = 10.0
 SCALE_ROW0 = 32
 HALF = N // 2
 CHUNK = N // 2
+SHARE = 64
 STEP = 128
 
 
@@ -60,13 +61,17 @@ def tile_attend_cosexp_topk_kernel(tc, qT, k_words, k_scales, rk, rq, offs, out)
         nc.sync.dma_start(word_pool[:], k_words[0].rearrange("p t b -> p (t b)").bitcast(I32))
 
         q_rows = qT[0].rearrange("(o p t) q -> o p t q", o=PASSES, t=4)
-        q_raw = []
-        for o in range(PASSES):
-            q_raw.append(turns.tile([P, 4, NQ], F32, name="q_raw%d" % o, align_bytes=256, offset=12288 + 4096 * o))
-        nc.sync.dma_start(q_raw[0][:], q_rows[0])
-        nc.sync.dma_start(q_raw[1][:, 0:2, :], q_rows[1][:, 0:2, :])
+        q_raw0 = turns.tile([P, 4, NQ], F32, name="q_raw0", align_bytes=256, offset=12288)
+        nc.sync.dma_start(q_raw0[:], q_rows[0])
+        q_in = {(0, c): q_raw0[:, :, c * P : (c + 1) * P] for c in range(TILES)}
 
-        gain = sb.tile([P, 1], F32, name="gain", tag="gain", align_bytes=256)
+        def load_pass1(c):
+            q_in[1, c] = turns.tile([P, 4, P], F32, name="q_raw1%d" % c, align_bytes=256, offset=16384 + 2048 * c)[:]
+            nc.sync.dma_start(q_in[1, c], q_rows[1][:, :, c * P : (c + 1) * P])
+
+        load_pass1(0)
+
+        gain = turns.tile([P, 1], F32, name="gain", align_bytes=256, offset=5120)
         nc.scalar.activation(gain[:], minus_gain[:], ACT.Exp, scale=-math.log(GAIN) / GAIN)
 
         listed_scales = sb.tile([P, N], U8, name="listed_scales", align_bytes=256)
@@ -74,13 +79,11 @@ def tile_attend_cosexp_topk_kernel(tc, qT, k_words, k_scales, rk, rq, offs, out)
 
         rq_turned = ps.tile([P, P], F32, name="rq_turned", tag="bank1")
         nc.tensor.transpose(rq_turned[:], rq_rows[:, 0:P], ident[:])
-        rq_cols = sb.tile([P, TILES], F32, name="rq_cols")
-        nc.scalar.copy(rq_cols[:], rq_turned[:, P - TILES : P])
 
         rk_spread = [ps.tile([P, HALF], F32, name="rk_spread%d" % h) for h in range(2)]
         rk_cols = []
         for h in range(2):
-            rk_listed = q_raw[1][:, 3, :] if h == 0 else turns.tile([P, HALF], F32, name="rk_listed1", align_bytes=256, offset=512)[:]
+            rk_listed = turns.tile([P, HALF], F32, name="rk_listed%d" % h, align_bytes=256, offset=(18432, 512)[h])[:]
             listed = rk_pool[:].indirect(offsets[:, h * HALF // 16 : (h + 1) * HALF // 16])
             if h == 0:
                 nc.scalar.activation(rk_listed, listed, ACT.Copy)
@@ -90,7 +93,7 @@ def tile_attend_cosexp_topk_kernel(tc, qT, k_words, k_scales, rk, rq, offs, out)
             for s in range(HALF // P):
                 nc.tensor.transpose(rk_turned[:, s, :], rk_listed[:, s * P : (s + 1) * P], ident[:])
             rk_cols.append(turns.tile([P, HALF // P], F32, name="rk_cols%d" % h, align_bytes=256, offset=(4096, 3072)[h]))
-            nc.scalar.activation(rk_cols[h][:], rk_turned[:, :, P - 1], ACT.Copy, scale=gain[:])
+            nc.scalar.copy(rk_cols[h][:], rk_turned[:, :, P - 1])
         for s in range(N // P):
             column = rk_cols[s * P // HALF][:, s % (HALF // P) : s % (HALF // P) + 1]
             nc.tensor.transpose(rk_spread[s * P // HALF][:, s * P % HALF : s * P % HALF + P], column.to_broadcast([P, P]), ident[:])
@@ -102,7 +105,7 @@ def tile_attend_cosexp_topk_kernel(tc, qT, k_words, k_scales, rk, rq, offs, out)
                 k_scale[32 * u : 32 * u + 4, 0 : PASSES * N].bitcast(I32), listed_scales[first : first + 8, :].bitcast(I32)
             )
 
-        nc.sync.dma_start(q_raw[1][:, 2:4, :], q_rows[1][:, 2:4, :])
+        load_pass1(1)
 
         listed_words = turns.tile([P, N], U32, name="listed_words", align_bytes=256, offset=20480)
         for h in range(2):
@@ -128,7 +131,7 @@ def tile_attend_cosexp_topk_kernel(tc, qT, k_words, k_scales, rk, rq, offs, out)
         def cast(copy, o, c, queries):
             copy(
                 q_bf[o, c][:, queries, :].rearrange("p (g i) t -> p g t i", i=4),
-                q_raw[o][:, :, c * P + queries.start : c * P + queries.stop].rearrange("p t (g i) -> p g t i", i=4),
+                q_in[o, c][:, :, queries].rearrange("p t (g i) -> p g t i", i=4),
             )
 
         def quantize(o, c, offset):
@@ -136,18 +139,21 @@ def tile_attend_cosexp_topk_kernel(tc, qT, k_words, k_scales, rk, rq, offs, out)
             q_scale[o, c] = sb.tile([P, P], U8, name="q_scale%d%d" % (o, c), align_bytes=256)
             nc.vector.quantize_mx(q_codes[o, c][:].bitcast(FP8X4), q_scale[o, c][:], q_bf[o, c][:].rearrange("p q t -> p (q t)"))
 
-        for o, c, offset in ((0, 0, 0), (0, 1, 1024), (1, 0, 13312), (1, 1, 3072)):
+        for o, c, offset in ((0, 0, 0), (0, 1, 1280), (1, 0, 5120), (1, 1, 3072)):
             q_bf[o, c] = turns.tile([P, P, 4], BF16, name="q_bf%d%d" % (o, c), align_bytes=256, offset=offset)
         cast(nc.scalar.copy, 0, 0, slice(0, P))
+        rq_cols = turns.tile([P, TILES], F32, name="rq_cols", align_bytes=256, offset=1024)
+        nc.scalar.activation(rq_cols[:], rq_turned[:, P - TILES : P], ACT.Copy, scale=gain[:])
         cast(nc.scalar.copy, 0, 1, slice(0, P))
         copy_rk(0, 12288)
         quantize(0, 0, 8192)
-        quantize(0, 1, 8704)
         cast(nc.vector.tensor_copy, 1, 0, slice(0, P))
-        cast(nc.scalar.copy, 1, 1, slice(0, P))
-        quantize(1, 0, 9216)
+        quantize(0, 1, 8704)
+        quantize(1, 0, 13312)
+        cast(nc.vector.tensor_copy, 1, 1, slice(0, SHARE))
+        cast(nc.scalar.copy, 1, 1, slice(SHARE, P))
         quantize(1, 1, 9728)
-        copy_rk(1, 16384)
+        copy_rk(1, 19456)
 
         pieces = ((0, 0, STEP, "bank2"), (0, STEP, STEP, "bank4"), (0, CHUNK, CHUNK, "bank3"), (1, 0, CHUNK, "bank0"), (1, CHUNK, CHUNK, "bank1"))
         scores = {}
@@ -171,7 +177,10 @@ def tile_attend_cosexp_topk_kernel(tc, qT, k_words, k_scales, rk, rq, offs, out)
 
         for c in range(TILES):
             for u in range(N // CHUNK):
-                scaled = sb.tile([P, CHUNK], F32, name="scaled%d%d" % (c, u), align_bytes=256)
+                if c + u == 0:
+                    scaled = turns.tile([P, CHUNK], F32, name="scaled00", align_bytes=256, offset=18432)
+                else:
+                    scaled = sb.tile([P, CHUNK], F32, name="scaled%d%d" % (c, u), align_bytes=256)
                 result = sb.tile([P, CHUNK], F32, name="result%d%d" % (c, u), align_bytes=256)
                 for s in range(0, CHUNK, STEP):
                     nc.vector.tensor_tensor(scaled[:, s : s + STEP], scores[c, u * CHUNK + s], rk_rows[u][:, s : s + STEP], MULT)

@@ -155,36 +155,45 @@ def tile_attend_cosexp_topk_kernel(tc, qT, k_words, k_scales, rk, rq, offs, out)
         quantize(1, 1, 9728)
         copy_rk(1, 19456)
 
-        pieces = ((0, 0, STEP, "bank2"), (0, STEP, STEP, "bank4"), (0, CHUNK, CHUNK, "bank3"), (1, 0, CHUNK, "bank0"), (1, CHUNK, CHUNK, "bank1"))
         scores = {}
-        for c, first, width, tag in pieces:
-            bank = ps.tile([P, width], F32, name="scores%d_%d" % (c, first), tag=tag)
-            for s in range(0, width, STEP):
-                scores[c, first + s] = bank[:, s : s + STEP]
-            scores[c, first, width] = bank[:]
 
-        for o in range(PASSES):
-            for c, first, width, tag in pieces:
-                nc.tensor.matmul_mx(
-                    scores[c, first, width],
-                    lhsT=q_codes[o, c][:].bitcast(FP8X4),
-                    lhsT_scale=q_scale[o, c][:],
-                    rhs=k_codes[:, o, first : first + width].bitcast(FP4X4),
-                    rhs_scale=k_scale[:, o * N + first : o * N + first + width],
-                    start=o == 0,
-                    stop=o == PASSES - 1,
+        def matmul(o, c, first, width, tag=None):
+            if o == 0:
+                bank = ps.tile([P, width], F32, name="scores%d_%d" % (c, first), tag=tag)
+                scores[c, first, width] = bank[:]
+                for s in range(0, width, STEP):
+                    scores[c, first + s] = bank[:, s : s + STEP]
+            nc.tensor.matmul_mx(
+                scores[c, first, width],
+                lhsT=q_codes[o, c][:].bitcast(FP8X4),
+                lhsT_scale=q_scale[o, c][:],
+                rhs=k_codes[:, o, first : first + width].bitcast(FP4X4),
+                rhs_scale=k_scale[:, o * N + first : o * N + first + width],
+                start=o == 0,
+                stop=o == PASSES - 1,
+            )
+
+        def epilogue(c, u):
+            if c + u == 0:
+                scaled = turns.tile([P, CHUNK], F32, name="scaled00", align_bytes=256, offset=18432)
+            else:
+                scaled = sb.tile([P, CHUNK], F32, name="scaled%d%d" % (c, u), align_bytes=256)
+            result = sb.tile([P, CHUNK], F32, name="result%d%d" % (c, u), align_bytes=256)
+            for s in range(0, CHUNK, STEP):
+                nc.vector.tensor_tensor(scaled[:, s : s + STEP], scores[c, u * CHUNK + s], rk_rows[u][:, s : s + STEP], MULT)
+                nc.scalar.activation(
+                    result[:, s : s + STEP], scaled[:, s : s + STEP], ACT.Exp, bias=minus_gain[:], scale=rq_cols[:, c : c + 1]
                 )
+            nc.sync.dma_start(out[0, c * P : (c + 1) * P, u * CHUNK : (u + 1) * CHUNK], result[:])
 
-        for c in range(TILES):
-            for u in range(N // CHUNK):
-                if c + u == 0:
-                    scaled = turns.tile([P, CHUNK], F32, name="scaled00", align_bytes=256, offset=18432)
-                else:
-                    scaled = sb.tile([P, CHUNK], F32, name="scaled%d%d" % (c, u), align_bytes=256)
-                result = sb.tile([P, CHUNK], F32, name="result%d%d" % (c, u), align_bytes=256)
-                for s in range(0, CHUNK, STEP):
-                    nc.vector.tensor_tensor(scaled[:, s : s + STEP], scores[c, u * CHUNK + s], rk_rows[u][:, s : s + STEP], MULT)
-                    nc.scalar.activation(
-                        result[:, s : s + STEP], scaled[:, s : s + STEP], ACT.Exp, bias=minus_gain[:], scale=rq_cols[:, c : c + 1]
-                    )
-                nc.sync.dma_start(out[0, c * P : (c + 1) * P, u * CHUNK : (u + 1) * CHUNK], result[:])
+        pieces = ((0, 0, STEP, "bank2"), (0, STEP, STEP, "bank4"), (0, CHUNK, CHUNK, "bank3"), (1, 0, CHUNK, "bank0"))
+        for o in range(PASSES):
+            for piece in pieces:
+                matmul(o, *piece)
+        epilogue(0, 0)
+        for o in range(PASSES):
+            matmul(o, 1, CHUNK, STEP, "bank2")
+            matmul(o, 1, CHUNK + STEP, STEP, "bank4")
+        epilogue(0, 1)
+        epilogue(1, 0)
+        epilogue(1, 1)

@@ -25,6 +25,7 @@ GAIN = 10.0
 SCALE_ROW0 = 32
 HALF = N // 2
 CHUNK = N // 2
+FIRST_SHARE = 48
 SHARE = 64
 STEP = 128
 
@@ -113,12 +114,16 @@ def tile_attend_cosexp_topk_kernel(tc, qT, k_words, k_scales, rk, rq, offs, out)
                 listed_words[:, h * HALF : (h + 1) * HALF],
                 word_pool[:].bitcast(U32).indirect(offsets[:, h * HALF // 16 : (h + 1) * HALF // 16]),
             )
-        k_codes = sb.tile([P, PASSES, N], U16, name="k_codes", align_bytes=256)
-        for h in range(2):
-            nc.vector.tensor_copy(
-                k_codes[:, :, h * HALF : (h + 1) * HALF],
-                listed_words[:, h * HALF : (h + 1) * HALF].bitcast(U16).rearrange("p (n o) -> p o n", o=PASSES),
-            )
+        by_pass = listed_words[:].bitcast(U16).rearrange("p (n o) -> p o n", o=PASSES)
+        k_first = sb.tile([P, PASSES, HALF], U16, name="k_first", align_bytes=256)
+        nc.vector.tensor_copy(k_first[:], by_pass[:, :, 0:HALF])
+        k_codes = {(o, 0): k_first[:, o, :] for o in range(PASSES)}
+
+        def part_second_half(o, offset):
+            k_codes[o, 1] = turns.tile([P, HALF], U16, name="k_second%d" % o, align_bytes=256, offset=offset)[:]
+            nc.vector.tensor_copy(k_codes[o, 1], by_pass[:, o, HALF:N])
+
+        part_second_half(0, 10240)
 
         rk_rows = {}
 
@@ -144,12 +149,14 @@ def tile_attend_cosexp_topk_kernel(tc, qT, k_words, k_scales, rk, rq, offs, out)
         cast(nc.scalar.copy, 0, 0, slice(0, P))
         rq_cols = turns.tile([P, TILES], F32, name="rq_cols", align_bytes=256, offset=1024)
         nc.scalar.activation(rq_cols[:], rq_turned[:, P - TILES : P], ACT.Copy, scale=gain[:])
-        cast(nc.scalar.copy, 0, 1, slice(0, P))
+        cast(nc.vector.tensor_copy, 0, 1, slice(0, FIRST_SHARE))
+        cast(nc.scalar.copy, 0, 1, slice(FIRST_SHARE, P))
         copy_rk(0, 12288)
         quantize(0, 0, 8192)
         cast(nc.vector.tensor_copy, 1, 0, slice(0, P))
         quantize(0, 1, 8704)
         quantize(1, 0, 13312)
+        part_second_half(1, 16384)
         cast(nc.vector.tensor_copy, 1, 1, slice(0, SHARE))
         cast(nc.scalar.copy, 1, 1, slice(SHARE, P))
         quantize(1, 1, 9728)
@@ -167,7 +174,7 @@ def tile_attend_cosexp_topk_kernel(tc, qT, k_words, k_scales, rk, rq, offs, out)
                 scores[c, first, width],
                 lhsT=q_codes[o, c][:].bitcast(FP8X4),
                 lhsT_scale=q_scale[o, c][:],
-                rhs=k_codes[:, o, first : first + width].bitcast(FP4X4),
+                rhs=k_codes[o, first // HALF][:, first % HALF : first % HALF + width].bitcast(FP4X4),
                 rhs_scale=k_scale[:, o * N + first : o * N + first + width],
                 start=o == 0,
                 stop=o == PASSES - 1,

@@ -27,6 +27,7 @@ HALF = N // 2
 CHUNK = N // 2
 FIRST_SHARE = 48
 SHARE = 64
+ZERO_SPLIT = 1408
 STEP = 128
 
 
@@ -42,8 +43,8 @@ def tile_attend_cosexp_topk_kernel(tc, qT, k_words, k_scales, rk, rq, offs, out)
 
         ident = sb.tile([P, P], F32, name="ident", tag="ident", align_bytes=256)
         make_identity(nc, ident[:])
-        rk_pool = turns.tile([P, T], F32, name="rk_pool", align_bytes=256, offset=20480)
-        nc.gpsimd.memset(rk_pool[0 : P - 1, :], 0.0)
+        rk_pool = turns.tile([P, T + 1], F32, name="rk_pool", align_bytes=256, offset=20480)
+        nc.gpsimd.memset(rk_pool[0 : P - 1, 0:ZERO_SPLIT], 0.0)
         minus_gain = sb.tile([P, 1], F32, name="minus_gain")
         nc.vector.memset(minus_gain[:], -GAIN)
 
@@ -52,7 +53,8 @@ def tile_attend_cosexp_topk_kernel(tc, qT, k_words, k_scales, rk, rq, offs, out)
         nc.vector.memset(scale_pool[0:SCALE_ROW0, :].bitcast(I32), 0)
         nc.vector.memset(scale_pool[2 * SCALE_ROW0 : P, :].bitcast(I32), 0)
 
-        nc.sync.dma_start(rk_pool[P - 1 : P, :], rk[0:1, :])
+        nc.vector.memset(rk_pool[0 : P - 1, ZERO_SPLIT : T + 1], 0.0)
+        nc.sync.dma_start(rk_pool[P - 1 : P, 0:T], rk[0:1, :])
 
         rq_rows = sb.tile([P, P + 1], F32, name="rq_rows", align_bytes=256)
         nc.vector.memset(rq_rows[0 : P - TILES, :], 0.0)
@@ -85,7 +87,7 @@ def tile_attend_cosexp_topk_kernel(tc, qT, k_words, k_scales, rk, rq, offs, out)
         rk_cols = []
         for h in range(2):
             rk_listed = turns.tile([P, HALF], F32, name="rk_listed%d" % h, align_bytes=256, offset=(18432, 512)[h])[:]
-            listed = rk_pool[:].indirect(offsets[:, h * HALF // 16 : (h + 1) * HALF // 16])
+            listed = rk_pool[:, 0:T].indirect(offsets[:, h * HALF // 16 : (h + 1) * HALF // 16])
             if h == 0:
                 nc.scalar.activation(rk_listed, listed, ACT.Copy)
             else:

@@ -27,7 +27,7 @@ HALF = N // 2
 CHUNK = N // 2
 FIRST_SHARE = 48
 SHARE = 64
-ZERO_SPLIT = 1408
+ZERO_SPLIT = 1664
 STEP = 128
 
 
@@ -39,7 +39,6 @@ def tile_attend_cosexp_topk_kernel(tc, qT, k_words, k_scales, rk, rq, offs, out)
         ps = ctx.enter_context(tc.psum_pool(name="ps", bufs=1))
 
         offsets = sb.tile([P, N // 16], U16, name="offsets", align_bytes=256)
-        nc.sync.dma_start(offsets[:], offs)
 
         ident = sb.tile([P, P], F32, name="ident", tag="ident", align_bytes=256)
         make_identity(nc, ident[:])
@@ -50,11 +49,12 @@ def tile_attend_cosexp_topk_kernel(tc, qT, k_words, k_scales, rk, rq, offs, out)
 
         scale_pool = sb.tile([P, T + 4], U8, name="scale_pool", tag="scale_pool", align_bytes=256)
         nc.sync.dma_start(scale_pool[SCALE_ROW0 : 2 * SCALE_ROW0, 0:T].bitcast(I32), k_scales.bitcast(I32).rearrange("o f t -> f o t"))
+        nc.sync.dma_start(offsets[:], offs)
         nc.vector.memset(scale_pool[0:SCALE_ROW0, :].bitcast(I32), 0)
         nc.vector.memset(scale_pool[2 * SCALE_ROW0 : P, :].bitcast(I32), 0)
 
         nc.vector.memset(rk_pool[0 : P - 1, ZERO_SPLIT : T + 1], 0.0)
-        nc.sync.dma_start(rk_pool[P - 1 : P, 0:T], rk[0:1, :])
+        nc.scalar.dma_start(rk_pool[P - 1 : P, 0:T], rk[0:1, :])
 
         rq_rows = sb.tile([P, P + 1], F32, name="rq_rows", align_bytes=256)
         nc.vector.memset(rq_rows[0 : P - TILES, :], 0.0)

import math
from contextlib import ExitStack

import concourse.mybir as mybir
from concourse.masks import make_identity

N, T, D, NQ = 512, 2048, 1024, 256
FLOPS = 2 * NQ * N * D

F32 = mybir.dt.float32
BF16 = mybir.dt.bfloat16
I32 = mybir.dt.int32
U32 = mybir.dt.uint32
U16 = mybir.dt.uint16
U8 = mybir.dt.uint8
FP8X4 = mybir.dt.float8_e4m3fn_x4
FP4X4 = mybir.dt.float4_e2m1fn_x4
ACT = mybir.ActivationFunctionType
MULT = mybir.AluOpType.mult

P = 128
PASSES = D // 512
TILES = NQ // P
GAIN = 10.0
SCALE_ROW0 = 32
HALF = N // 2
CHUNK = N // 2
FIRST_SHARE = 48
SHARE = 64
ZERO_SPLIT = 1664
STEP = 128


def tile_attend_cosexp_topk_kernel(tc, qT, k_words, k_scales, rk, rq, offs, out):
    nc = tc.nc
    with ExitStack() as ctx:
        sb = ctx.enter_context(tc.tile_pool(name="sb", bufs=1))
        turns = ctx.enter_context(tc.tile_pool(name="turns", bufs=1))
        ps = ctx.enter_context(tc.psum_pool(name="ps", bufs=1))

        offsets = sb.tile([P, N // 16], U16, name="offsets", align_bytes=256)

        ident = sb.tile([P, P], F32, name="ident", tag="ident", align_bytes=256)
        make_identity(nc, ident[:])
        rk_pool = turns.tile([P, T + 1], F32, name="rk_pool", align_bytes=256, offset=20480)
        nc.gpsimd.memset(rk_pool[0 : P - 1, 0:ZERO_SPLIT], 0.0)
        minus_gain = sb.tile([P, 1], F32, name="minus_gain")
        nc.vector.memset(minus_gain[:], -GAIN)

        scale_pool = sb.tile([P, T + 4], U8, name="scale_pool", tag="scale_pool", align_bytes=256)
        nc.sync.dma_start(scale_pool[SCALE_ROW0 : 2 * SCALE_ROW0, 0:T].bitcast(I32), k_scales.bitcast(I32).rearrange("o f t -> f o t"))
        nc.sync.dma_start(offsets[:], offs)
        nc.vector.memset(scale_pool[0:SCALE_ROW0, :].bitcast(I32), 0)
        nc.vector.memset(scale_pool[2 * SCALE_ROW0 : P, :].bitcast(I32), 0)

        nc.vector.memset(rk_pool[0 : P - 1, ZERO_SPLIT : T + 1], 0.0)
        nc.scalar.dma_start(rk_pool[P - 1 : P, 0:T], rk[0:1, :])

        rq_rows = sb.tile([P, P + 1], F32, name="rq_rows", align_bytes=256)
        nc.vector.memset(rq_rows[0 : P - TILES, :], 0.0)
        nc.scalar.dma_start(rq_rows[P - TILES : P, 0:P], rq[0].rearrange("(c q) one -> c (q one)", c=TILES))

        word_pool = sb.tile([P, T], I32, name="word_pool", tag="word_pool", align_bytes=256)
        nc.sync.dma_start(word_pool[:], k_words[0].rearrange("p t b -> p (t b)").bitcast(I32))

        q_rows = qT[0].rearrange("(o p t) q -> o p t q", o=PASSES, t=4)
        q_raw0 = turns.tile([P, 4, NQ], F32, name="q_raw0", align_bytes=256, offset=12288)
        nc.sync.dma_start(q_raw0[:], q_rows[0])
        q_in = {(0, c): q_raw0[:, :, c * P : (c + 1) * P] for c in range(TILES)}

        def load_pass1(c):
            q_in[1, c] = turns.tile([P, 4, P], F32, name="q_raw1%d" % c, align_bytes=256, offset=16384 + 2048 * c)[:]
            nc.sync.dma_start(q_in[1, c], q_rows[1][:, :, c * P : (c + 1) * P])

        load_pass1(0)

        gain = turns.tile([P, 1], F32, name="gain", align_bytes=256, offset=5120)
        nc.scalar.activation(gain[:], minus_gain[:], ACT.Exp, scale=-math.log(GAIN) / GAIN)

        listed_scales = sb.tile([P, N], U8, name="listed_scales", align_bytes=256)
        nc.vector.tensor_copy(listed_scales[:], scale_pool[:, 0:T].indirect(offsets[:]))

        rq_turned = ps.tile([P, P], F32, name="rq_turned", tag="bank1")
        nc.tensor.transpose(rq_turned[:], rq_rows[:, 0:P], ident[:])

        rk_spread = [ps.tile([P, HALF], F32, name="rk_spread%d" % h) for h in range(2)]
        rk_cols = []
        for h in range(2):
            rk_listed = turns.tile([P, HALF], F32, name="rk_listed%d" % h, align_bytes=256, offset=(18432, 512)[h])[:]
            listed = rk_pool[:, 0:T].indirect(offsets[:, h * HALF // 16 : (h + 1) * HALF // 16])
            if h == 0:
                nc.scalar.activation(rk_listed, listed, ACT.Copy)
            else:
                nc.vector.tensor_copy(rk_listed, listed)
            rk_turned = ps.tile([P, HALF // P, P], F32, name="rk_turned%d" % h, tag="bank%d" % (2 * h))
            for s in range(HALF // P):
                nc.tensor.transpose(rk_turned[:, s, :], rk_listed[:, s * P : (s + 1) * P], ident[:])
            rk_cols.append(turns.tile([P, HALF // P], F32, name="rk_cols%d" % h, align_bytes=256, offset=(4096, 3072)[h]))
            nc.scalar.copy(rk_cols[h][:], rk_turned[:, :, P - 1])
        for s in range(N // P):
            column = rk_cols[s * P // HALF][:, s % (HALF // P) : s % (HALF // P) + 1]
            nc.tensor.transpose(rk_spread[s * P // HALF][:, s * P % HALF : s * P % HALF + P], column.to_broadcast([P, P]), ident[:])

        k_scale = sb.tile([P, PASSES * N], U8, name="k_scale", align_bytes=256)
        for u in range(4):
            first = SCALE_ROW0 + 8 * u
            nc.sync.dma_start(
                k_scale[32 * u : 32 * u + 4, 0 : PASSES * N].bitcast(I32), listed_scales[first : first + 8, :].bitcast(I32)
            )

        load_pass1(1)

        listed_words = turns.tile([P, N], U32, name="listed_words", align_bytes=256, offset=20480)
        for h in range(2):
            nc.vector.tensor_copy(
                listed_words[:, h * HALF : (h + 1) * HALF],
                word_pool[:].bitcast(U32).indirect(offsets[:, h * HALF // 16 : (h + 1) * HALF // 16]),
            )
        by_pass = listed_words[:].bitcast(U16).rearrange("p (n o) -> p o n", o=PASSES)
        k_first = sb.tile([P, PASSES, HALF], U16, name="k_first", align_bytes=256)
        nc.vector.tensor_copy(k_first[:], by_pass[:, :, 0:HALF])
        k_codes = {(o, 0): k_first[:, o, :] for o in range(PASSES)}

        def part_second_half(o, offset):
            k_codes[o, 1] = turns.tile([P, HALF], U16, name="k_second%d" % o, align_bytes=256, offset=offset)[:]
            nc.vector.tensor_copy(k_codes[o, 1], by_pass[:, o, HALF:N])

        part_second_half(0, 10240)

        rk_rows = {}

        def copy_rk(h, offset):
            rk_rows[h] = turns.tile([P, HALF], F32, name="rk_rows%d" % h, align_bytes=256, offset=offset)
            nc.scalar.copy(rk_rows[h][:], rk_spread[h][:])

        q_bf, q_codes, q_scale = {}, {}, {}

        def cast(copy, o, c, queries):
            copy(
                q_bf[o, c][:, queries, :].rearrange("p (g i) t -> p g t i", i=4),
                q_in[o, c][:, :, queries].rearrange("p t (g i) -> p g t i", i=4),
            )

        def quantize(o, c, offset):
            q_codes[o, c] = turns.tile([P, P], U32, name="q_codes%d%d" % (o, c), align_bytes=256, offset=offset)
            q_scale[o, c] = sb.tile([P, P], U8, name="q_scale%d%d" % (o, c), align_bytes=256)
            nc.vector.quantize_mx(q_codes[o, c][:].bitcast(FP8X4), q_scale[o, c][:], q_bf[o, c][:].rearrange("p q t -> p (q t)"))

        for o, c, offset in ((0, 0, 0), (0, 1, 1280), (1, 0, 5120), (1, 1, 3072)):
            q_bf[o, c] = turns.tile([P, P, 4], BF16, name="q_bf%d%d" % (o, c), align_bytes=256, offset=offset)
        cast(nc.scalar.copy, 0, 0, slice(0, P))
        rq_cols = turns.tile([P, TILES], F32, name="rq_cols", align_bytes=256, offset=1024)
        nc.scalar.activation(rq_cols[:], rq_turned[:, P - TILES : P], ACT.Copy, scale=gain[:])
        cast(nc.vector.tensor_copy, 0, 1, slice(0, FIRST_SHARE))
        cast(nc.scalar.copy, 0, 1, slice(FIRST_SHARE, P))
        copy_rk(0, 12288)
        quantize(0, 0, 8192)
        cast(nc.vector.tensor_copy, 1, 0, slice(0, P))
        quantize(0, 1, 8704)
        quantize(1, 0, 13312)
        part_second_half(1, 16384)
        cast(nc.vector.tensor_copy, 1, 1, slice(0, SHARE))
        cast(nc.scalar.copy, 1, 1, slice(SHARE, P))
        quantize(1, 1, 9728)
        copy_rk(1, 19456)

        scores = {}

        def matmul(o, c, first, width, tag=None):
            if o == 0:
                bank = ps.tile([P, width], F32, name="scores%d_%d" % (c, first), tag=tag)
                scores[c, first, width] = bank[:]
                for s in range(0, width, STEP):
                    scores[c, first + s] = bank[:, s : s + STEP]
            nc.tensor.matmul_mx(
                scores[c, first, width],
                lhsT=q_codes[o, c][:].bitcast(FP8X4),
                lhsT_scale=q_scale[o, c][:],
                rhs=k_codes[o, first // HALF][:, first % HALF : first % HALF + width].bitcast(FP4X4),
                rhs_scale=k_scale[:, o * N + first : o * N + first + width],
                start=o == 0,
                stop=o == PASSES - 1,
            )

        def epilogue(c, u):
            if c + u == 0:
                scaled = turns.tile([P, CHUNK], F32, name="scaled00", align_bytes=256, offset=18432)
            else:
                scaled = sb.tile([P, CHUNK], F32, name="scaled%d%d" % (c, u), align_bytes=256)
            result = sb.tile([P, CHUNK], F32, name="result%d%d" % (c, u), align_bytes=256)
            for s in range(0, CHUNK, STEP):
                nc.vector.tensor_tensor(scaled[:, s : s + STEP], scores[c, u * CHUNK + s], rk_rows[u][:, s : s + STEP], MULT)
                nc.scalar.activation(
                    result[:, s : s + STEP], scaled[:, s : s + STEP], ACT.Exp, bias=minus_gain[:], scale=rq_cols[:, c : c + 1]
                )
            nc.sync.dma_start(out[0, c * P : (c + 1) * P, u * CHUNK : (u + 1) * CHUNK], result[:])

        pieces = ((0, 0, STEP, "bank2"), (0, STEP, STEP, "bank4"), (0, CHUNK, CHUNK, "bank3"), (1, 0, CHUNK, "bank0"))
        for o in range(PASSES):
            for piece in pieces:
                matmul(o, *piece)
        epilogue(0, 0)
        for o in range(PASSES):
            matmul(o, 1, CHUNK, STEP, "bank2")
            matmul(o, 1, CHUNK + STEP, STEP, "bank4")
        epilogue(0, 1)
        epilogue(1, 0)
        epilogue(1, 1)
